import numpy as np
import ml_dtypes


def mxq(x, axis, fmt="e4m3"):
    dtype, down = {"e4m3": (ml_dtypes.float8_e4m3fn, 7), "e5m2": (ml_dtypes.float8_e5m2, 14)}[fmt]
    v = np.moveaxis(np.asarray(x, np.float32).astype(ml_dtypes.bfloat16).astype(np.float64), axis, -1)
    blocks = v.reshape(v.shape[:-1] + (-1, 32))
    amax = np.abs(blocks).max(-1, keepdims=True)
    byte = np.maximum(np.where(amax > 0, np.frexp(amax)[1] - 1 + 127, 0) - down, 1)
    scale = np.exp2(byte - 127.0)
    codes = (blocks / scale).astype(np.float32).astype(dtype).astype(np.float64)
    return np.moveaxis((codes * scale).reshape(v.shape), -1, axis)


WIDE = False


def mx_kscale(k):
    if not WIDE:
        return np.ones(k)
    levels = np.array([10, -10, 5, -5, 0])
    if k % 512:
        return np.exp2(np.random.permutation(np.resize(levels, k // 32))).repeat(32)
    a = np.empty((k // 512, 16))
    for p in range(k // 512):
        a[p, :8] = np.random.permutation(np.resize(levels, 8))
        for g in range(8):
            far = levels[np.abs(levels - a[p, g]) >= 10]
            a[p, g + 8] = far[np.random.randint(len(far))]
    return np.exp2(a.ravel()).repeat(32)


def f64(x):
    return np.asarray(x).astype(np.float64)


def striped(idx):
    return np.tile(idx.reshape(-1, 16).T, (8, 1)).astype(np.uint16)


def unstriped(offs):
    return offs[:16].T.reshape(-1).astype(np.int64)


def pack_weight(w):
    k, n = w.shape
    w = f64(np.asarray(w, np.float32).astype(ml_dtypes.bfloat16)).reshape(k // 32, 32, n)
    amax = np.abs(w).max(1)
    byte = np.clip(np.where(amax > 0, np.frexp(amax)[1] - 1 + 127 - 7, 1), 1, 254)
    scaled = (w * np.exp2(127.0 - byte)[:, None, :]).reshape(k, n).astype(np.float32)
    words = np.ascontiguousarray(scaled.reshape(k // 512, 128, 4, n).transpose(0, 1, 3, 2)).astype(ml_dtypes.float8_e4m3fn).view(np.uint8)
    return words, np.ascontiguousarray(byte.astype(np.uint8).reshape(k // 512, 16, n))


def unpack_weight(words, scales):
    g, p, n, _ = words.shape
    vals = np.ascontiguousarray(words).view(ml_dtypes.float8_e4m3fn).astype(np.float64) * np.repeat(np.exp2(scales.astype(np.float64) - 127.0), 8, axis=1)[..., None]
    return vals.transpose(0, 1, 3, 2).reshape(g * 512, n)


def relu(v):
    return np.maximum(v, 0.0)


K, T, S, V, N = 512, 4096, 1536, 512, 256
P = 2 ** 7


def setup_inputs():
    n = np.random.standard_normal
    s = mx_kscale(K)[:, None]
    packed_w1 = pack_weight(n((K, N)) / np.sqrt(K) / s)
    return {
        "xT": (n((K, T)) * s).astype(np.float32),
        "w1_words": packed_w1[0],
        "w1_scales": packed_w1[1],
        "margin": np.tile(np.random.uniform(0.2, 2.0, V), (P, 1)).astype(np.float32),
        "offs": striped(np.random.permutation(T)[:S]),
    }


def reference(xT, w1_words, w1_scales, margin, offs):
    xq = mxq(f64(xT)[:, unstriped(offs)], 0, "e4m3")
    h = unpack_weight(w1_words, w1_scales).T @ xq
    near = (h[:, :V] - h[:, V:2 * V]) ** 2
    far = (h[:, :V] - h[:, 2 * V:3 * V]) ** 2
    return relu(near - far + f64(margin)[:1])

@@ -1,0 +1,117 @@
+from contextlib import ExitStack
+
+import concourse.mybir as mybir
+
+K, T, S, V, N = 512, 4096, 1536, 512, 256
+P = 128
+FLOPS = 2 * K * N * S
+
+F32 = mybir.dt.float32
+BF16 = mybir.dt.bfloat16
+I32 = mybir.dt.int32
+U32 = mybir.dt.uint32
+U16 = mybir.dt.uint16
+U8 = mybir.dt.uint8
+FP8X4 = mybir.dt.float8_e4m3fn_x4
+ACT = mybir.ActivationFunctionType
+ALU = mybir.AluOpType
+
+CHUNKS = [[4096], [4096], [2048, 1024, 1024], [2048, 1536, 512]]
+
+
+def tile_picked_triplet_none_e_kernel(tc, xT, w1_words, w1_scales, margin, offs, out):
+    nc = tc.nc
+    with ExitStack() as ctx:
+        keep = ctx.enter_context(tc.tile_pool(name="keep", bufs=1))
+        psum = ctx.enter_context(tc.psum_pool(name="psum", bufs=1))
+
+        offsets = keep.tile([P, S // 16], U16, name="offsets")
+        w_words = keep.tile([P, N], U32, name="w_words", align_bytes=64)
+        w_scales = keep.tile([P, N], U8, name="w_scales", align_bytes=64)
+        margins = keep.tile([P, V], F32, name="margins")
+        planes = [keep.tile([P, T], F32, name=f"plane{j}") for j in range(4)]
+        rounded = [keep.tile([P, T], BF16, name=f"rounded{j}") for j in range(4)]
+        picked = [keep.tile([P, V, 4], BF16, name=f"picked{i}", align_bytes=64) for i in range(3)]
+        codes = [keep.tile([P, V], U32, name=f"codes{i}", align_bytes=64) for i in range(3)]
+        scales = [keep.tile([P, V], U8, name=f"scales{i}", align_bytes=64) for i in range(3)]
+
+        nc.vector.memset(w_scales[:].bitcast(I32), 0)
+        rows = xT.rearrange("(p j) t -> j p t", j=4)
+        for j in range(4):
+            c0 = 0
+            for n_chunk, width in enumerate(CHUNKS[j]):
+                nc.sync.dma_start(out=planes[j][:, c0 : c0 + width], in_=rows[j][:, c0 : c0 + width])
+                c0 = c0 + width
+                if j == 0 and n_chunk == 0:
+                    nc.sync.dma_start(offsets[:], offs)
+            if j == 0:
+                for q in range(4):
+                    nc.sync.dma_start(
+                        out=w_scales[32 * q : 32 * q + 4, :].bitcast(I32),
+                        in_=w1_scales[0, 4 * q : 4 * q + 4, :].bitcast(I32),
+                    )
+        nc.sync.dma_start(out=w_words[:].bitcast(I32), in_=w1_words[0].rearrange("p n t -> p (n t)").bitcast(I32))
+        nc.sync.dma_start(out=margins[:], in_=margin)
+
+        def third(i):
+            return offsets[:, 32 * i : 32 * (i + 1)]
+
+        for j in range(4):
+            c0 = 0
+            for n_chunk, width in enumerate(CHUNKS[j]):
+                cols = slice(c0, c0 + width)
+                if j == 0 and n_chunk == 0:
+                    nc.scalar.activation(out=rounded[j][:, cols], in_=planes[j][:, cols], func=ACT.Copy)
+                else:
+                    nc.vector.tensor_copy(out=rounded[j][:, cols], in_=planes[j][:, cols])
+                c0 = c0 + width
+            nc.vector.tensor_copy(out=picked[0][:, :, j], in_=planes[j][:].indirect(third(0)))
+            for i in (1, 2):
+                nc.scalar.activation(out=picked[i][:, :, j], in_=rounded[j][:].indirect(third(i)), func=ACT.Copy)
+
+        h = {}
+
+        def quantise(i):
+            nc.vector.quantize_mx(
+                out=codes[i][:].bitcast(FP8X4), scales=scales[i][:], in_=picked[i][:].rearrange("p v j -> p (v j)")
+            )
+
+        def project(i, mt):
+            cols = slice(P * mt, P * (mt + 1))
+            acc = psum.tile([P, V], F32, name=f"h{i}{mt}")
+            nc.tensor.matmul_mx(
+                out=acc[:], lhsT=w_words[:, cols].bitcast(FP8X4), lhsT_scale=w_scales[:, cols],
+                rhs=codes[i][:].bitcast(FP8X4), rhs_scale=scales[i][:], start=True, stop=True,
+            )
+            h[i, mt] = acc
+
+        anchors = [keep.tile([P, V], F32, name=f"anchor{mt}") for mt in range(2)]
+        d1 = [keep.tile([P, V], F32, name=f"d1_{mt}") for mt in range(2)]
+        d2 = [keep.tile([P, V], F32, name=f"d2_{mt}") for mt in range(2)]
+        near = [keep.tile([P, V], F32, name=f"near{mt}") for mt in range(2)]
+        far = [keep.tile([P, V], F32, name=f"far{mt}") for mt in range(2)]
+        nm = [keep.tile([P, V], F32, name=f"nm{mt}") for mt in range(2)]
+        loss = [keep.tile([P, V], F32, name=f"loss{mt}") for mt in range(2)]
+        res = [keep.tile([P, V], F32, name=f"res{mt}") for mt in range(2)]
+        quantise(0)
+        quantise(1)
+        for mt in range(2):
+            project(0, mt)
+            project(1, mt)
+        nc.vector.tensor_copy(out=anchors[0][:], in_=h[0, 0][:])
+        quantise(2)
+        project(2, 0)
+        project(2, 1)
+        nc.scalar.copy(out=anchors[1][:], in_=h[0, 1][:])
+        for mt in range(2):
+            nc.vector.tensor_tensor(out=d1[mt][:], in0=h[1, mt][:], in1=anchors[mt][:], op=ALU.subtract)
+            nc.scalar.activation(out=near[mt][:], in_=d1[mt][:], func=ACT.Square)
+        nc.vector.tensor_tensor(out=nm[0][:], in0=near[0][:], in1=margins[:], op=ALU.add)
+        for mt in range(2):
+            nc.vector.tensor_tensor(out=d2[mt][:], in0=h[2, mt][:], in1=anchors[mt][:], op=ALU.subtract)
+            nc.scalar.activation(out=far[mt][:], in_=d2[mt][:], func=ACT.Square)
+        nc.vector.tensor_tensor(out=nm[1][:], in0=near[1][:], in1=margins[:], op=ALU.add)
+        for mt, c0, c1 in ((0, 0, 512), (1, 0, 256), (1, 256, 512)):
+            nc.vector.tensor_tensor(out=loss[mt][:, c0:c1], in0=nm[mt][:, c0:c1], in1=far[mt][:, c0:c1], op=ALU.subtract)
+            nc.scalar.activation(out=res[mt][:, c0:c1], in_=loss[mt][:, c0:c1], func=ACT.Relu)
+            nc.sync.dma_start(out=out[P * mt : P * (mt + 1), c0:c1], in_=res[mt][:, c0:c1])

@@ -16,7 +16,7 @@ FP8X4 = mybir.dt.float8_e4m3fn_x4
 ACT = mybir.ActivationFunctionType
 ALU = mybir.AluOpType
 
-CHUNKS = [[4096], [4096], [2048, 1024, 1024], [2048, 1536, 512]]
+CHUNKS = [[1024, 2048, 1024], [2048, 1024, 1024], [2048, 1024, 1024], [2048, 1024, 512, 512]]
 
 
 def tile_picked_triplet_none_e_kernel(tc, xT, w1_words, w1_scales, margin, offs, out):
@@ -106,12 +106,17 @@ def tile_picked_triplet_none_e_kernel(tc, xT, w1_words, w1_scales, margin, offs,
         for mt in range(2):
             nc.vector.tensor_tensor(out=d1[mt][:], in0=h[1, mt][:], in1=anchors[mt][:], op=ALU.subtract)
             nc.scalar.activation(out=near[mt][:], in_=d1[mt][:], func=ACT.Square)
-        nc.vector.tensor_tensor(out=nm[0][:], in0=near[0][:], in1=margins[:], op=ALU.add)
+        nc.gpsimd.tensor_tensor(out=nm[0][:], in0=near[0][:], in1=margins[:], op=ALU.add)
         for mt in range(2):
             nc.vector.tensor_tensor(out=d2[mt][:], in0=h[2, mt][:], in1=anchors[mt][:], op=ALU.subtract)
             nc.scalar.activation(out=far[mt][:], in_=d2[mt][:], func=ACT.Square)
         nc.vector.tensor_tensor(out=nm[1][:], in0=near[1][:], in1=margins[:], op=ALU.add)
-        for mt, c0, c1 in ((0, 0, 512), (1, 0, 256), (1, 256, 512)):
-            nc.vector.tensor_tensor(out=loss[mt][:, c0:c1], in0=nm[mt][:, c0:c1], in1=far[mt][:, c0:c1], op=ALU.subtract)
-            nc.scalar.activation(out=res[mt][:, c0:c1], in_=loss[mt][:, c0:c1], func=ACT.Relu)
-            nc.sync.dma_start(out=out[P * mt : P * (mt + 1), c0:c1], in_=res[mt][:, c0:c1])
+        nc.vector.tensor_tensor(out=loss[0][:], in0=nm[0][:], in1=far[0][:], op=ALU.subtract)
+        nc.scalar.activation(out=res[0][:], in_=loss[0][:], func=ACT.Relu)
+        nc.sync.dma_start(out=out[0:P, :], in_=res[0][:])
+        halves = (slice(0, V // 2), slice(V // 2, V))
+        for cols in halves:
+            nc.vector.tensor_tensor(out=loss[1][:, cols], in0=nm[1][:, cols], in1=far[1][:, cols], op=ALU.subtract)
+        for cols, queue in zip(halves, (nc.sync, nc.scalar)):
+            nc.vector.tensor_scalar(out=res[1][:, cols], in0=loss[1][:, cols], scalar1=0.0, scalar2=None, op0=ALU.max)
+            queue.dma_start(out=out[P : 2 * P, cols], in_=res[1][:, cols])

@@ -16,7 +16,7 @@ FP8X4 = mybir.dt.float8_e4m3fn_x4
 ACT = mybir.ActivationFunctionType
 ALU = mybir.AluOpType
 
-CHUNKS = [[1024, 2048, 1024], [2048, 1024, 1024], [2048, 1024, 1024], [2048, 1024, 512, 512]]
+CHUNKS = [[2048, 2048], [2048, 2048], [2048, 1024, 1024], [2048, 1024, 512, 512]]
 
 
 def tile_picked_triplet_none_e_kernel(tc, xT, w1_words, w1_scales, margin, offs, out):
@@ -62,6 +62,10 @@ def tile_picked_triplet_none_e_kernel(tc, xT, w1_words, w1_scales, margin, offs,
                 cols = slice(c0, c0 + width)
                 if j == 0 and n_chunk == 0:
                     nc.scalar.activation(out=rounded[j][:, cols], in_=planes[j][:, cols], func=ACT.Copy)
+                elif j == 3 and n_chunk == len(CHUNKS[j]) - 1:
+                    mid = c0 + width // 2
+                    nc.vector.tensor_copy(out=rounded[j][:, c0:mid], in_=planes[j][:, c0:mid])
+                    nc.scalar.activation(out=rounded[j][:, mid:], in_=planes[j][:, mid:], func=ACT.Copy)
                 else:
                     nc.vector.tensor_copy(out=rounded[j][:, cols], in_=planes[j][:, cols])
                 c0 = c0 + width
@@ -106,10 +110,11 @@ def tile_picked_triplet_none_e_kernel(tc, xT, w1_words, w1_scales, margin, offs,
         for mt in range(2):
             nc.vector.tensor_tensor(out=d1[mt][:], in0=h[1, mt][:], in1=anchors[mt][:], op=ALU.subtract)
             nc.scalar.activation(out=near[mt][:], in_=d1[mt][:], func=ACT.Square)
-        nc.gpsimd.tensor_tensor(out=nm[0][:], in0=near[0][:], in1=margins[:], op=ALU.add)
+        nc.gpsimd.tensor_tensor(out=nm[0][:, :256], in0=near[0][:, :256], in1=margins[:, :256], op=ALU.add)
         for mt in range(2):
             nc.vector.tensor_tensor(out=d2[mt][:], in0=h[2, mt][:], in1=anchors[mt][:], op=ALU.subtract)
             nc.scalar.activation(out=far[mt][:], in_=d2[mt][:], func=ACT.Square)
+        nc.vector.tensor_tensor(out=nm[0][:, 256:], in0=near[0][:, 256:], in1=margins[:, 256:], op=ALU.add)
         nc.vector.tensor_tensor(out=nm[1][:], in0=near[1][:], in1=margins[:], op=ALU.add)
         nc.vector.tensor_tensor(out=loss[0][:], in0=nm[0][:], in1=far[0][:], op=ALU.subtract)
         nc.scalar.activation(out=res[0][:], in_=loss[0][:], func=ACT.Relu)

@@ -4,6 +4,9 @@ import concourse.mybir as mybir
 
 K, T, S, V, N = 512, 4096, 1536, 512, 256
 P = 128
+PACK = 4
+LIST_ROWS = 16
+ANCHOR, POSITIVE, NEGATIVE = 0, 1, 2
 FLOPS = 2 * K * N * S
 
 F32 = mybir.dt.float32
@@ -17,6 +20,8 @@ ACT = mybir.ActivationFunctionType
 ALU = mybir.AluOpType
 
 CHUNKS = [[2048, 2048], [2048, 2048], [2048, 1024, 1024], [2048, 1024, 512, 512]]
+LAST_CAST_ON_VECTOR = 320
+MARGIN_ON_GPSIMD = 256
 
 
 def tile_picked_triplet_none_e_kernel(tc, xT, w1_words, w1_scales, margin, offs, out):
@@ -25,27 +30,27 @@ def tile_picked_triplet_none_e_kernel(tc, xT, w1_words, w1_scales, margin, offs,
         keep = ctx.enter_context(tc.tile_pool(name="keep", bufs=1))
         psum = ctx.enter_context(tc.psum_pool(name="psum", bufs=1))
 
-        offsets = keep.tile([P, S // 16], U16, name="offsets")
+        offsets = keep.tile([P, S // LIST_ROWS], U16, name="offsets")
         w_words = keep.tile([P, N], U32, name="w_words", align_bytes=64)
         w_scales = keep.tile([P, N], U8, name="w_scales", align_bytes=64)
         margins = keep.tile([P, V], F32, name="margins")
-        planes = [keep.tile([P, T], F32, name=f"plane{j}") for j in range(4)]
-        rounded = [keep.tile([P, T], BF16, name=f"rounded{j}") for j in range(4)]
-        picked = [keep.tile([P, V, 4], BF16, name=f"picked{i}", align_bytes=64) for i in range(3)]
+        planes = [keep.tile([P, T], F32, name=f"plane{j}") for j in range(PACK)]
+        rounded = [keep.tile([P, T], BF16, name=f"rounded{j}") for j in range(PACK)]
+        picked = [keep.tile([P, V, PACK], BF16, name=f"picked{i}", align_bytes=64) for i in range(3)]
         codes = [keep.tile([P, V], U32, name=f"codes{i}", align_bytes=64) for i in range(3)]
         scales = [keep.tile([P, V], U8, name=f"scales{i}", align_bytes=64) for i in range(3)]
 
         nc.vector.memset(w_scales[:].bitcast(I32), 0)
-        rows = xT.rearrange("(p j) t -> j p t", j=4)
-        for j in range(4):
+        rows = xT.rearrange("(p j) t -> j p t", j=PACK)
+        for j in range(PACK):
             c0 = 0
-            for n_chunk, width in enumerate(CHUNKS[j]):
+            for width in CHUNKS[j]:
                 nc.sync.dma_start(out=planes[j][:, c0 : c0 + width], in_=rows[j][:, c0 : c0 + width])
-                c0 = c0 + width
-                if j == 0 and n_chunk == 0:
+                if j == 0 and c0 == 0:
                     nc.sync.dma_start(offsets[:], offs)
+                c0 = c0 + width
             if j == 0:
-                for q in range(4):
+                for q in range(P // 32):
                     nc.sync.dma_start(
                         out=w_scales[32 * q : 32 * q + 4, :].bitcast(I32),
                         in_=w1_scales[0, 4 * q : 4 * q + 4, :].bitcast(I32),
@@ -54,74 +59,100 @@ def tile_picked_triplet_none_e_kernel(tc, xT, w1_words, w1_scales, margin, offs,
         nc.sync.dma_start(out=margins[:], in_=margin)
 
         def third(i):
-            return offsets[:, 32 * i : 32 * (i + 1)]
+            return offsets[:, i * V // LIST_ROWS : (i + 1) * V // LIST_ROWS]
 
-        for j in range(4):
+        for j in range(PACK):
             c0 = 0
-            for n_chunk, width in enumerate(CHUNKS[j]):
-                cols = slice(c0, c0 + width)
-                if j == 0 and n_chunk == 0:
-                    nc.scalar.activation(out=rounded[j][:, cols], in_=planes[j][:, cols], func=ACT.Copy)
-                elif j == 3 and n_chunk == len(CHUNKS[j]) - 1:
-                    mid = c0 + width // 2
+            for width in CHUNKS[j]:
+                c1 = c0 + width
+                if j == 0 and c0 == 0:
+                    nc.scalar.activation(out=rounded[j][:, c0:c1], in_=planes[j][:, c0:c1], func=ACT.Copy)
+                elif j == PACK - 1 and c1 == T:
+                    mid = c0 + LAST_CAST_ON_VECTOR
                     nc.vector.tensor_copy(out=rounded[j][:, c0:mid], in_=planes[j][:, c0:mid])
-                    nc.scalar.activation(out=rounded[j][:, mid:], in_=planes[j][:, mid:], func=ACT.Copy)
+                    nc.scalar.activation(out=rounded[j][:, mid:c1], in_=planes[j][:, mid:c1], func=ACT.Copy)
                 else:
-                    nc.vector.tensor_copy(out=rounded[j][:, cols], in_=planes[j][:, cols])
-                c0 = c0 + width
-            nc.vector.tensor_copy(out=picked[0][:, :, j], in_=planes[j][:].indirect(third(0)))
-            for i in (1, 2):
+                    nc.vector.tensor_copy(out=rounded[j][:, c0:c1], in_=planes[j][:, c0:c1])
+                c0 = c1
+            nc.vector.tensor_copy(out=picked[ANCHOR][:, :, j], in_=planes[j][:].indirect(third(ANCHOR)))
+            for i in (POSITIVE, NEGATIVE):
                 nc.scalar.activation(out=picked[i][:, :, j], in_=rounded[j][:].indirect(third(i)), func=ACT.Copy)
 
         h = {}
 
-        def quantise(i):
+        def quantise(i, v0=0, v1=V):
             nc.vector.quantize_mx(
-                out=codes[i][:].bitcast(FP8X4), scales=scales[i][:], in_=picked[i][:].rearrange("p v j -> p (v j)")
+                out=codes[i][:, v0:v1].bitcast(FP8X4),
+                scales=scales[i][:, v0:v1],
+                in_=picked[i][:, v0:v1, :].rearrange("p v j -> p (v j)"),
             )
 
-        def project(i, mt):
-            cols = slice(P * mt, P * (mt + 1))
-            acc = psum.tile([P, V], F32, name=f"h{i}{mt}")
-            nc.tensor.matmul_mx(
-                out=acc[:], lhsT=w_words[:, cols].bitcast(FP8X4), lhsT_scale=w_scales[:, cols],
-                rhs=codes[i][:].bitcast(FP8X4), rhs_scale=scales[i][:], start=True, stop=True,
-            )
-            h[i, mt] = acc
+        def project(i, ft, width=V):
+            features = slice(P * ft, P * (ft + 1))
+            acc = psum.tile([P, V], F32, name=f"h{i}{ft}")
+            for v0 in range(0, V, width):
+                samples = slice(v0, v0 + width)
+                nc.tensor.matmul_mx(
+                    out=acc[:, samples],
+                    lhsT=w_words[:, features].bitcast(FP8X4),
+                    lhsT_scale=w_scales[:, features],
+                    rhs=codes[i][:, samples].bitcast(FP8X4),
+                    rhs_scale=scales[i][:, samples],
+                    start=True,
+                    stop=True,
+                )
+            h[i, ft] = acc
 
-        anchors = [keep.tile([P, V], F32, name=f"anchor{mt}") for mt in range(2)]
-        d1 = [keep.tile([P, V], F32, name=f"d1_{mt}") for mt in range(2)]
-        d2 = [keep.tile([P, V], F32, name=f"d2_{mt}") for mt in range(2)]
-        near = [keep.tile([P, V], F32, name=f"near{mt}") for mt in range(2)]
-        far = [keep.tile([P, V], F32, name=f"far{mt}") for mt in range(2)]
-        nm = [keep.tile([P, V], F32, name=f"nm{mt}") for mt in range(2)]
-        loss = [keep.tile([P, V], F32, name=f"loss{mt}") for mt in range(2)]
-        res = [keep.tile([P, V], F32, name=f"res{mt}") for mt in range(2)]
-        quantise(0)
-        quantise(1)
-        for mt in range(2):
-            project(0, mt)
-            project(1, mt)
-        nc.vector.tensor_copy(out=anchors[0][:], in_=h[0, 0][:])
-        quantise(2)
-        project(2, 0)
-        project(2, 1)
-        nc.scalar.copy(out=anchors[1][:], in_=h[0, 1][:])
-        for mt in range(2):
-            nc.vector.tensor_tensor(out=d1[mt][:], in0=h[1, mt][:], in1=anchors[mt][:], op=ALU.subtract)
-            nc.scalar.activation(out=near[mt][:], in_=d1[mt][:], func=ACT.Square)
-        nc.gpsimd.tensor_tensor(out=nm[0][:, :256], in0=near[0][:, :256], in1=margins[:, :256], op=ALU.add)
-        for mt in range(2):
-            nc.vector.tensor_tensor(out=d2[mt][:], in0=h[2, mt][:], in1=anchors[mt][:], op=ALU.subtract)
-            nc.scalar.activation(out=far[mt][:], in_=d2[mt][:], func=ACT.Square)
-        nc.vector.tensor_tensor(out=nm[0][:, 256:], in0=near[0][:, 256:], in1=margins[:, 256:], op=ALU.add)
-        nc.vector.tensor_tensor(out=nm[1][:], in0=near[1][:], in1=margins[:], op=ALU.add)
-        nc.vector.tensor_tensor(out=loss[0][:], in0=nm[0][:], in1=far[0][:], op=ALU.subtract)
-        nc.scalar.activation(out=res[0][:], in_=loss[0][:], func=ACT.Relu)
-        nc.sync.dma_start(out=out[0:P, :], in_=res[0][:])
+        def tiles(name):
+            return [keep.tile([P, V], F32, name=f"{name}{ft}") for ft in range(N // P)]
+
+        anchors = tiles("anchors")
+        to_positive = tiles("to_positive")
+        to_negative = tiles("to_negative")
+        near = tiles("near")
+        far = tiles("far")
+        near_margin = tiles("near_margin")
+        loss = tiles("loss")
+        result = tiles("result")
+
+        quantise(ANCHOR, 0, V // 2)
+        quantise(ANCHOR, V // 2, V)
+        quantise(POSITIVE)
+        project(ANCHOR, 0, V // 2)
+        project(POSITIVE, 0)
+        project(ANCHOR, 1)
+        project(POSITIVE, 1)
+
+        nc.vector.tensor_copy(out=anchors[0][:], in_=h[ANCHOR, 0][:])
+        quantise(NEGATIVE)
+        project(NEGATIVE, 0)
+        project(NEGATIVE, 1)
+        nc.scalar.copy(out=anchors[1][:], in_=h[ANCHOR, 1][:])
+
+        for ft in range(N // P):
+            nc.vector.tensor_tensor(out=to_positive[ft][:], in0=h[POSITIVE, ft][:], in1=anchors[ft][:], op=ALU.subtract)
+            nc.scalar.activation(out=near[ft][:], in_=to_positive[ft][:], func=ACT.Square)
+        on_gpsimd = slice(0, MARGIN_ON_GPSIMD)
+        on_vector = slice(MARGIN_ON_GPSIMD, V)
+        nc.gpsimd.tensor_tensor(
+            out=near_margin[0][:, on_gpsimd], in0=near[0][:, on_gpsimd], in1=margins[:, on_gpsimd], op=ALU.add
+        )
+        for ft in range(N // P):
+            nc.vector.tensor_tensor(out=to_negative[ft][:], in0=h[NEGATIVE, ft][:], in1=anchors[ft][:], op=ALU.subtract)
+            nc.scalar.activation(out=far[ft][:], in_=to_negative[ft][:], func=ACT.Square)
+        nc.vector.tensor_tensor(
+            out=near_margin[0][:, on_vector], in0=near[0][:, on_vector], in1=margins[:, on_vector], op=ALU.add
+        )
+        nc.vector.tensor_tensor(out=near_margin[1][:], in0=near[1][:], in1=margins[:], op=ALU.add)
+
+        nc.vector.tensor_tensor(out=loss[0][:], in0=near_margin[0][:], in1=far[0][:], op=ALU.subtract)
+        nc.scalar.activation(out=result[0][:], in_=loss[0][:], func=ACT.Relu)
+        nc.sync.dma_start(out=out[0:P, :], in_=result[0][:])
         halves = (slice(0, V // 2), slice(V // 2, V))
         for cols in halves:
-            nc.vector.tensor_tensor(out=loss[1][:, cols], in0=nm[1][:, cols], in1=far[1][:, cols], op=ALU.subtract)
+            nc.vector.tensor_tensor(
+                out=loss[1][:, cols], in0=near_margin[1][:, cols], in1=far[1][:, cols], op=ALU.subtract
+            )
         for cols, queue in zip(halves, (nc.sync, nc.scalar)):
-            nc.vector.tensor_scalar(out=res[1][:, cols], in0=loss[1][:, cols], scalar1=0.0, scalar2=None, op0=ALU.max)
-            queue.dma_start(out=out[P : 2 * P, cols], in_=res[1][:, cols])
+            nc.vector.tensor_scalar(out=result[1][:, cols], in0=loss[1][:, cols], scalar1=0.0, scalar2=None, op0=ALU.max)
+            queue.dma_start(out=out[P : 2 * P, cols], in_=result[1][:, cols])

@@ -76,9 +76,7 @@ def tile_picked_triplet_none_e_kernel(tc, xT, w1_words, w1_scales, margin, offs,
                 c0 = c1
             nc.vector.tensor_copy(out=picked[ANCHOR][:, :, j], in_=planes[j][:].indirect(third(ANCHOR)))
             for i in (POSITIVE, NEGATIVE):
-                nc.scalar.activation(out=picked[i][:, :, j], in_=rounded[j][:].indirect(third(i)), func=ACT.Copy)
-
-        h = {}
+                nc.scalar.activation(out=picked[i][:, :, j], in_=rounded[j][:].indirect(third(i)), func=ACT.Copy, scale=-1.0)
 
         def quantise(i, v0=0, v1=V):
             nc.vector.quantize_mx(
@@ -87,72 +85,74 @@ def tile_picked_triplet_none_e_kernel(tc, xT, w1_words, w1_scales, margin, offs,
                 in_=picked[i][:, v0:v1, :].rearrange("p v j -> p (v j)"),
             )
 
-        def project(i, ft, width=V):
+        def project(acc, i, ft, cols, start, stop):
             features = slice(P * ft, P * (ft + 1))
-            acc = psum.tile([P, V], F32, name=f"h{i}{ft}")
-            for v0 in range(0, V, width):
-                samples = slice(v0, v0 + width)
-                nc.tensor.matmul_mx(
-                    out=acc[:, samples],
-                    lhsT=w_words[:, features].bitcast(FP8X4),
-                    lhsT_scale=w_scales[:, features],
-                    rhs=codes[i][:, samples].bitcast(FP8X4),
-                    rhs_scale=scales[i][:, samples],
-                    start=True,
-                    stop=True,
-                )
-            h[i, ft] = acc
+            nc.tensor.matmul_mx(
+                out=acc[:, cols],
+                lhsT=w_words[:, features].bitcast(FP8X4),
+                lhsT_scale=w_scales[:, features],
+                rhs=codes[i][:, cols].bitcast(FP8X4),
+                rhs_scale=scales[i][:, cols],
+                start=start,
+                stop=stop,
+            )
 
-        def tiles(name):
-            return [keep.tile([P, V], F32, name=f"{name}{ft}") for ft in range(N // P)]
+        def tiles(pool, name):
+            return [pool.tile([P, V], F32, name=f"{name}{ft}") for ft in range(N // P)]
 
-        anchors = tiles("anchors")
-        to_positive = tiles("to_positive")
-        to_negative = tiles("to_negative")
-        near = tiles("near")
-        far = tiles("far")
-        near_margin = tiles("near_margin")
-        loss = tiles("loss")
-        result = tiles("result")
+        H = V // 2
+        lo, hi, every = slice(0, H), slice(H, V), slice(0, V)
+        to_pos = tiles(psum, "to_pos")
+        to_neg = tiles(psum, "to_neg")
+        alone = psum.tile([P, H], F32, name="alone")
+        pos_alone = psum.tile([P, H], F32, name="pos_alone")
+        neg_alone = psum.tile([P, H], F32, name="neg_alone")
+        anchors = keep.tile([P, H], F32, name="anchors")
+        d_pos = keep.tile([P, H], F32, name="d_pos")
+        d_neg = keep.tile([P, H], F32, name="d_neg")
+        near = tiles(keep, "near")
+        far = tiles(keep, "far")
+        near_margin = tiles(keep, "near_margin")
+        loss = tiles(keep, "loss")
+        result = tiles(keep, "result")
 
-        quantise(ANCHOR, 0, V // 2)
-        quantise(ANCHOR, V // 2, V)
+        quantise(ANCHOR, 0, H)
+        quantise(ANCHOR, H, V)
+        project(alone, ANCHOR, 0, lo, True, True)
+        project(to_pos[0], ANCHOR, 0, hi, True, False)
+        project(to_pos[1], ANCHOR, 1, every, True, False)
         quantise(POSITIVE)
-        project(ANCHOR, 0, V // 2)
-        project(POSITIVE, 0)
-        project(ANCHOR, 1)
-        project(POSITIVE, 1)
+        nc.vector.tensor_copy(out=anchors[:], in_=alone[:])
+        project(pos_alone, POSITIVE, 0, lo, True, True)
+        project(to_pos[0], POSITIVE, 0, hi, False, True)
+        project(to_pos[1], POSITIVE, 1, every, False, True)
+        project(to_neg[0], ANCHOR, 0, hi, True, False)
+        project(to_neg[1], ANCHOR, 1, every, True, False)
+        nc.vector.tensor_tensor(out=d_pos[:], in0=pos_alone[:], in1=anchors[:], op=ALU.add)
+        quantise(NEGATIVE, 0, H)
+        quantise(NEGATIVE, H, V)
+        project(neg_alone, NEGATIVE, 0, lo, True, True)
+        project(to_neg[0], NEGATIVE, 0, hi, False, True)
+        project(to_neg[1], NEGATIVE, 1, every, False, True)
 
-        nc.vector.tensor_copy(out=anchors[0][:], in_=h[ANCHOR, 0][:])
-        quantise(NEGATIVE)
-        project(NEGATIVE, 0)
-        project(NEGATIVE, 1)
-        nc.scalar.copy(out=anchors[1][:], in_=h[ANCHOR, 1][:])
-
-        for ft in range(N // P):
-            nc.vector.tensor_tensor(out=to_positive[ft][:], in0=h[POSITIVE, ft][:], in1=anchors[ft][:], op=ALU.subtract)
-            nc.scalar.activation(out=near[ft][:], in_=to_positive[ft][:], func=ACT.Square)
-        on_gpsimd = slice(0, MARGIN_ON_GPSIMD)
-        on_vector = slice(MARGIN_ON_GPSIMD, V)
-        nc.gpsimd.tensor_tensor(
-            out=near_margin[0][:, on_gpsimd], in0=near[0][:, on_gpsimd], in1=margins[:, on_gpsimd], op=ALU.add
-        )
-        for ft in range(N // P):
-            nc.vector.tensor_tensor(out=to_negative[ft][:], in0=h[NEGATIVE, ft][:], in1=anchors[ft][:], op=ALU.subtract)
-            nc.scalar.activation(out=far[ft][:], in_=to_negative[ft][:], func=ACT.Square)
-        nc.vector.tensor_tensor(
-            out=near_margin[0][:, on_vector], in0=near[0][:, on_vector], in1=margins[:, on_vector], op=ALU.add
-        )
-        nc.vector.tensor_tensor(out=near_margin[1][:], in0=near[1][:], in1=margins[:], op=ALU.add)
+        nc.scalar.activation(out=near[0][:, lo], in_=d_pos[:], func=ACT.Square)
+        nc.scalar.activation(out=near[0][:, hi], in_=to_pos[0][:, hi], func=ACT.Square)
+        nc.scalar.activation(out=near[1][:], in_=to_pos[1][:], func=ACT.Square)
+        nc.vector.tensor_tensor(out=d_neg[:], in0=neg_alone[:], in1=anchors[:], op=ALU.add)
+        for ft in range(2):
+            nc.vector.tensor_tensor(out=near_margin[ft][:], in0=near[ft][:], in1=margins[:], op=ALU.add)
+        nc.scalar.activation(out=far[0][:, hi], in_=to_neg[0][:, hi], func=ACT.Square)
+        nc.scalar.activation(out=far[0][:, lo], in_=d_neg[:], func=ACT.Square)
+        nc.scalar.activation(out=far[1][:, lo], in_=to_neg[1][:, lo], func=ACT.Square)
+        nc.scalar.activation(out=far[1][:, hi], in_=to_neg[1][:, hi], func=ACT.Square)
 
         nc.vector.tensor_tensor(out=loss[0][:], in0=near_margin[0][:], in1=far[0][:], op=ALU.subtract)
         nc.scalar.activation(out=result[0][:], in_=loss[0][:], func=ACT.Relu)
         nc.sync.dma_start(out=out[0:P, :], in_=result[0][:])
-        halves = (slice(0, V // 2), slice(V // 2, V))
-        for cols in halves:
+        for cols in (lo, hi):
             nc.vector.tensor_tensor(
                 out=loss[1][:, cols], in0=near_margin[1][:, cols], in1=far[1][:, cols], op=ALU.subtract
             )
-        for cols, queue in zip(halves, (nc.sync, nc.scalar)):
+        for cols, queue in zip((lo, hi), (nc.sync, nc.scalar)):
             nc.vector.tensor_scalar(out=result[1][:, cols], in0=loss[1][:, cols], scalar1=0.0, scalar2=None, op0=ALU.max)
             queue.dma_start(out=out[P : 2 * P, cols], in_=result[1][:, cols])

@@ -1,6 +1,7 @@
 from contextlib import ExitStack
 
 import concourse.mybir as mybir
+from concourse.masks import make_identity
 
 K, T, S, V, N = 512, 4096, 1536, 512, 256
 P = 128
@@ -19,7 +20,7 @@ FP8X4 = mybir.dt.float8_e4m3fn_x4
 ACT = mybir.ActivationFunctionType
 ALU = mybir.AluOpType
 
-CHUNKS = [[2048, 2048], [2048, 2048], [2048, 1024, 1024], [2048, 1024, 512, 512]]
+CHUNKS = [[2048, 2048], [2048, 1024, 1024], [2048, 1024, 512, 512], [2048, 1024, 512, 256, 256]]
 LAST_CAST_ON_VECTOR = 320
 MARGIN_ON_GPSIMD = 256
 
@@ -33,12 +34,14 @@ def tile_picked_triplet_none_e_kernel(tc, xT, w1_words, w1_scales, margin, offs,
         offsets = keep.tile([P, S // LIST_ROWS], U16, name="offsets")
         w_words = keep.tile([P, N], U32, name="w_words", align_bytes=64)
         w_scales = keep.tile([P, N], U8, name="w_scales", align_bytes=64)
-        margins = keep.tile([P, V], F32, name="margins")
+        margins = keep.tile([P, V // P], F32, name="margins")
+        identity = keep.tile([P, P], F32, name="identity")
+        make_identity(nc, identity[:])
         planes = [keep.tile([P, T], F32, name=f"plane{j}") for j in range(PACK)]
         rounded = [keep.tile([P, T], BF16, name=f"rounded{j}") for j in range(PACK)]
         picked = [keep.tile([P, V, PACK], BF16, name=f"picked{i}", align_bytes=64) for i in range(3)]
-        codes = [keep.tile([P, V], U32, name=f"codes{i}", align_bytes=64) for i in range(3)]
-        scales = [keep.tile([P, V], U8, name=f"scales{i}", align_bytes=64) for i in range(3)]
+        words = keep.tile([P, 8 * P], U32, name="words", align_bytes=64)
+        scale_bytes = keep.tile([P, S], U8, name="scale_bytes", align_bytes=64)
 
         nc.vector.memset(w_scales[:].bitcast(I32), 0)
         rows = xT.rearrange("(p j) t -> j p t", j=PACK)
@@ -55,8 +58,9 @@ def tile_picked_triplet_none_e_kernel(tc, xT, w1_words, w1_scales, margin, offs,
                         out=w_scales[32 * q : 32 * q + 4, :].bitcast(I32),
                         in_=w1_scales[0, 4 * q : 4 * q + 4, :].bitcast(I32),
                     )
+        with nc.allow_non_contiguous_dma(reason="one margin to a partition"):
+            nc.sync.dma_start(out=margins[:], in_=margin[0].rearrange("(c p) -> p c", p=P))
         nc.sync.dma_start(out=w_words[:].bitcast(I32), in_=w1_words[0].rearrange("p n t -> p (n t)").bitcast(I32))
-        nc.sync.dma_start(out=margins[:], in_=margin)
 
         def third(i):
             return offsets[:, i * V // LIST_ROWS : (i + 1) * V // LIST_ROWS]
@@ -65,94 +69,114 @@ def tile_picked_triplet_none_e_kernel(tc, xT, w1_words, w1_scales, margin, offs,
             c0 = 0
             for width in CHUNKS[j]:
                 c1 = c0 + width
-                if j == 0 and c0 == 0:
+                if (j == 0 and c0 == 0) or (j == PACK - 1 and c1 == T):
                     nc.scalar.activation(out=rounded[j][:, c0:c1], in_=planes[j][:, c0:c1], func=ACT.Copy)
-                elif j == PACK - 1 and c1 == T:
-                    mid = c0 + LAST_CAST_ON_VECTOR
-                    nc.vector.tensor_copy(out=rounded[j][:, c0:mid], in_=planes[j][:, c0:mid])
-                    nc.scalar.activation(out=rounded[j][:, mid:c1], in_=planes[j][:, mid:c1], func=ACT.Copy)
                 else:
                     nc.vector.tensor_copy(out=rounded[j][:, c0:c1], in_=planes[j][:, c0:c1])
                 c0 = c1
-            nc.vector.tensor_copy(out=picked[ANCHOR][:, :, j], in_=planes[j][:].indirect(third(ANCHOR)))
-            for i in (POSITIVE, NEGATIVE):
-                nc.scalar.activation(out=picked[i][:, :, j], in_=rounded[j][:].indirect(third(i)), func=ACT.Copy, scale=-1.0)
+            nc.vector.tensor_copy(out=picked[POSITIVE][:, :, j], in_=planes[j][:].indirect(third(POSITIVE)))
+            for i, sign in ((ANCHOR, -1.0), (NEGATIVE, 1.0)):
+                nc.scalar.activation(out=picked[i][:, :, j], in_=rounded[j][:].indirect(third(i)), func=ACT.Copy, scale=sign)
+
+        first_chunk = {(POSITIVE, 0): 0, (POSITIVE, 1): 2, (ANCHOR, 0): 5, (ANCHOR, 1): 0, (NEGATIVE, 0): 4, (NEGATIVE, 1): 2}
+
+        def place(i, v):
+            return P * first_chunk[i, v // (V // 2)] + v % (V // 2)
 
         def quantise(i, v0=0, v1=V):
             nc.vector.quantize_mx(
-                out=codes[i][:, v0:v1].bitcast(FP8X4),
-                scales=scales[i][:, v0:v1],
+                out=words[:, place(i, v0) : place(i, v0) + v1 - v0].bitcast(FP8X4),
+                scales=scale_bytes[:, i * V + v0 : i * V + v1],
                 in_=picked[i][:, v0:v1, :].rearrange("p v j -> p (v j)"),
             )
 
-        def project(acc, i, ft, cols, start, stop):
-            features = slice(P * ft, P * (ft + 1))
+        def project(acc, i, c, start, stop):
             nc.tensor.matmul_mx(
-                out=acc[:, cols],
-                lhsT=w_words[:, features].bitcast(FP8X4),
-                lhsT_scale=w_scales[:, features],
-                rhs=codes[i][:, cols].bitcast(FP8X4),
-                rhs_scale=scales[i][:, cols],
+                out=acc,
+                lhsT=words[:, place(i, P * c) : place(i, P * c) + P].bitcast(FP8X4),
+                lhsT_scale=scale_bytes[:, i * V + P * c : i * V + P * (c + 1)],
+                rhs=w_words[:].bitcast(FP8X4),
+                rhs_scale=w_scales[:],
                 start=start,
                 stop=stop,
             )
 
-        def tiles(pool, name):
-            return [pool.tile([P, V], F32, name=f"{name}{ft}") for ft in range(N // P)]
+        def turn(acc, src, start, stop):
+            nc.tensor.matmul(out=acc, lhsT=src, rhs=identity[:], start=start, stop=stop, is_transpose=True)
 
         H = V // 2
-        lo, hi, every = slice(0, H), slice(H, V), slice(0, V)
-        to_pos = tiles(psum, "to_pos")
-        to_neg = tiles(psum, "to_neg")
-        alone = psum.tile([P, H], F32, name="alone")
-        pos_alone = psum.tile([P, H], F32, name="pos_alone")
-        neg_alone = psum.tile([P, H], F32, name="neg_alone")
-        anchors = keep.tile([P, H], F32, name="anchors")
-        d_pos = keep.tile([P, H], F32, name="d_pos")
-        d_neg = keep.tile([P, H], F32, name="d_neg")
-        near = tiles(keep, "near")
-        far = tiles(keep, "far")
-        near_margin = tiles(keep, "near_margin")
-        loss = tiles(keep, "loss")
-        result = tiles(keep, "result")
+        alone = [psum.tile([P, N], F32, name=f"alone{i}", tag=f"bank{i}") for i in range(3)]
+        pos1 = psum.tile([P, N], F32, name="pos1")
+        pos23 = psum.tile([P, 2, N], F32, name="pos23")
+        neg1 = psum.tile([P, N], F32, name="neg1")
+        neg23 = psum.tile([P, 2, N], F32, name="neg23")
+        turned01 = psum.tile([P, 2, 2 * P], F32, name="turned01")
+        positives = keep.tile([P, N], F32, name="positives")
+        partial = keep.tile([P, N], F32, name="partial")
+        apart = keep.tile([P, N], F32, name="apart")
+        summed = keep.tile([P, N], F32, name="summed")
+        near = keep.tile([P, 3, N], F32, name="near")
+        far = keep.tile([P, 3, N], F32, name="far")
+        loss = [keep.tile([P, N], F32, name=f"loss{c}") for c in range(4)]
+        result01 = keep.tile([P, 2, 2 * P], F32, name="result01")
+        result2 = keep.tile([P, 2, P], F32, name="result2")
+        result3 = keep.tile([P, 2, P], F32, name="result3")
 
+        for ft in range(2):
+            turn(turned01[:, ft, 0:P], margins[:, 0:1].to_broadcast([P, P]), ft == 0, False)
+
+        quantise(POSITIVE, 0, H)
+        quantise(POSITIVE, H, V)
+        project(alone[POSITIVE][:], POSITIVE, 0, True, True)
+        project(pos1[:], POSITIVE, 1, True, False)
+        project(pos23[:, 0, :], POSITIVE, 2, True, False)
+        nc.vector.tensor_copy(out=positives[:], in_=alone[POSITIVE][:])
         quantise(ANCHOR, 0, H)
+        project(alone[ANCHOR][:], ANCHOR, 0, True, True)
+        project(pos1[:], ANCHOR, 1, False, True)
+        project(pos23[:, 1, :], POSITIVE, 3, False, False)
         quantise(ANCHOR, H, V)
-        project(alone, ANCHOR, 0, lo, True, True)
-        project(to_pos[0], ANCHOR, 0, hi, True, False)
-        project(to_pos[1], ANCHOR, 1, every, True, False)
-        quantise(POSITIVE)
-        nc.vector.tensor_copy(out=anchors[:], in_=alone[:])
-        project(pos_alone, POSITIVE, 0, lo, True, True)
-        project(to_pos[0], POSITIVE, 0, hi, False, True)
-        project(to_pos[1], POSITIVE, 1, every, False, True)
-        project(to_neg[0], ANCHOR, 0, hi, True, False)
-        project(to_neg[1], ANCHOR, 1, every, True, False)
-        nc.vector.tensor_tensor(out=d_pos[:], in0=pos_alone[:], in1=anchors[:], op=ALU.add)
+        project(pos23[:, 0, :], ANCHOR, 2, False, False)
+        project(pos23[:, 1, :], ANCHOR, 3, False, True)
+        project(neg1[:], ANCHOR, 1, True, False)
+        project(neg23[:, 0, :], ANCHOR, 2, True, False)
+        project(neg23[:, 1, :], ANCHOR, 3, False, False)
+        nc.vector.scalar_tensor_tensor(
+            out=partial[:], in0=alone[ANCHOR][:], scalar=2.0, in1=positives[:], op0=ALU.mult, op1=ALU.add
+        )
         quantise(NEGATIVE, 0, H)
         quantise(NEGATIVE, H, V)
-        project(neg_alone, NEGATIVE, 0, lo, True, True)
-        project(to_neg[0], NEGATIVE, 0, hi, False, True)
-        project(to_neg[1], NEGATIVE, 1, every, False, True)
+        project(alone[NEGATIVE][:], NEGATIVE, 0, True, True)
+        project(neg1[:], NEGATIVE, 1, False, True)
+        project(neg23[:, 0, :], NEGATIVE, 2, False, False)
+        project(neg23[:, 1, :], NEGATIVE, 3, False, True)
 
-        nc.scalar.activation(out=near[0][:, lo], in_=d_pos[:], func=ACT.Square)
-        nc.scalar.activation(out=near[0][:, hi], in_=to_pos[0][:, hi], func=ACT.Square)
-        nc.scalar.activation(out=near[1][:], in_=to_pos[1][:], func=ACT.Square)
-        nc.vector.tensor_tensor(out=d_neg[:], in0=neg_alone[:], in1=anchors[:], op=ALU.add)
-        for ft in range(2):
-            nc.vector.tensor_tensor(out=near_margin[ft][:], in0=near[ft][:], in1=margins[:], op=ALU.add)
-        nc.scalar.activation(out=far[0][:, hi], in_=to_neg[0][:, hi], func=ACT.Square)
-        nc.scalar.activation(out=far[0][:, lo], in_=d_neg[:], func=ACT.Square)
-        nc.scalar.activation(out=far[1][:, lo], in_=to_neg[1][:, lo], func=ACT.Square)
-        nc.scalar.activation(out=far[1][:, hi], in_=to_neg[1][:, hi], func=ACT.Square)
+        nc.scalar.activation(out=near[:, 0, :], in_=pos1[:], func=ACT.Square)
+        nc.scalar.activation(out=near[:, 1:3, :], in_=pos23[:], func=ACT.Square)
+        nc.scalar.activation(out=far[:, 0, :], in_=neg1[:], func=ACT.Square)
+        nc.scalar.activation(out=far[:, 1, :], in_=neg23[:, 0, :], func=ACT.Square)
+        nc.scalar.activation(out=far[:, 2, :], in_=neg23[:, 1, :], func=ACT.Square)
 
-        nc.vector.tensor_tensor(out=loss[0][:], in0=near_margin[0][:], in1=far[0][:], op=ALU.subtract)
-        nc.scalar.activation(out=result[0][:], in_=loss[0][:], func=ACT.Relu)
-        nc.sync.dma_start(out=out[0:P, :], in_=result[0][:])
-        for cols in (lo, hi):
-            nc.vector.tensor_tensor(
-                out=loss[1][:, cols], in0=near_margin[1][:, cols], in1=far[1][:, cols], op=ALU.subtract
+        nc.vector.tensor_tensor(out=apart[:], in0=positives[:], in1=alone[NEGATIVE][:], op=ALU.subtract)
+        nc.vector.tensor_tensor(out=summed[:], in0=alone[NEGATIVE][:], in1=partial[:], op=ALU.add)
+        nc.vector.tensor_tensor(out=loss[0][:], in0=apart[:], in1=summed[:], op=ALU.mult)
+        for c in range(1, 4):
+            nc.vector.scalar_tensor_tensor(
+                out=loss[c][:], in0=near[:, c - 1, :], scalar=margins[:, c : c + 1], in1=far[:, c - 1, :],
+                op0=ALU.add, op1=ALU.subtract,
             )
-        for cols, queue in zip((lo, hi), (nc.sync, nc.scalar)):
-            nc.vector.tensor_scalar(out=result[1][:, cols], in0=loss[1][:, cols], scalar1=0.0, scalar2=None, op0=ALU.max)
-            queue.dma_start(out=out[P : 2 * P, cols], in_=result[1][:, cols])
+        rows_out = out.rearrange("(f p) v -> p f v", p=P)
+        for c in range(2):
+            for ft in range(2):
+                turn(turned01[:, ft, P * c : P * (c + 1)], loss[c][:, P * ft : P * (ft + 1)], False, c == 1 and ft == 1)
+        turned2 = psum.tile([P, 2, P], F32, name="turned2", tag="bank0")
+        turned3 = psum.tile([P, 2, P], F32, name="turned3", tag="bank1")
+        for acc, c in ((turned2, 2), (turned3, 3)):
+            for ft in range(2):
+                nc.tensor.transpose(acc[:, ft, :], loss[c][:, P * ft : P * (ft + 1)], identity[:])
+        nc.scalar.activation(out=result01[:], in_=turned01[:], func=ACT.Relu)
+        nc.sync.dma_start(out=rows_out[:, :, 0 : 2 * P], in_=result01[:])
+        nc.scalar.activation(out=result2[:], in_=turned2[:], func=ACT.Relu)
+        nc.scalar.dma_start(out=rows_out[:, :, 2 * P : 3 * P], in_=result2[:])
+        nc.vector.tensor_scalar(out=result3[:], in0=turned3[:], scalar1=0.0, scalar2=None, op0=ALU.max)
+        nc.sync.dma_start(out=rows_out[:, :, 3 * P : 4 * P], in_=result3[:])

@@ -122,8 +122,10 @@ def tile_picked_triplet_none_e_kernel(tc, xT, w1_words, w1_scales, margin, offs,
         result2 = keep.tile([P, 2, P], F32, name="result2")
         result3 = keep.tile([P, 2, P], F32, name="result3")
 
+        minus_margin = keep.tile([P, 1], F32, name="minus_margin")
+        nc.gpsimd.tensor_scalar(out=minus_margin[:], in0=margins[:, 0:1], scalar1=-1.0, scalar2=0.0, op0=ALU.mult, op1=ALU.add)
         for ft in range(2):
-            turn(turned01[:, ft, 0:P], margins[:, 0:1].to_broadcast([P, P]), ft == 0, False)
+            turn(turned01[:, ft, 0:P], minus_margin[:, 0:1].to_broadcast([P, P]), ft == 0, False)
 
         quantise(POSITIVE, 0, H)
         quantise(POSITIVE, H, V)
@@ -157,26 +159,31 @@ def tile_picked_triplet_none_e_kernel(tc, xT, w1_words, w1_scales, margin, offs,
         nc.scalar.activation(out=far[:, 1, :], in_=neg23[:, 0, :], func=ACT.Square)
         nc.scalar.activation(out=far[:, 2, :], in_=neg23[:, 1, :], func=ACT.Square)
 
-        nc.vector.tensor_tensor(out=apart[:], in0=positives[:], in1=alone[NEGATIVE][:], op=ALU.subtract)
+        for c in range(1, 4):
+            nc.vector.tensor_scalar(
+                out=loss[c][:], in0=near[:, c - 1, :], scalar1=margins[:, c : c + 1], scalar2=-1.0, op0=ALU.add, op1=ALU.mult
+            )
+        nc.vector.tensor_tensor(out=apart[:], in0=alone[NEGATIVE][:], in1=positives[:], op=ALU.subtract)
         nc.vector.tensor_tensor(out=summed[:], in0=alone[NEGATIVE][:], in1=partial[:], op=ALU.add)
         nc.vector.tensor_tensor(out=loss[0][:], in0=apart[:], in1=summed[:], op=ALU.mult)
-        for c in range(1, 4):
-            nc.vector.scalar_tensor_tensor(
-                out=loss[c][:], in0=near[:, c - 1, :], scalar=margins[:, c : c + 1], in1=far[:, c - 1, :],
-                op0=ALU.add, op1=ALU.subtract,
-            )
         rows_out = out.rearrange("(f p) v -> p f v", p=P)
-        for c in range(2):
-            for ft in range(2):
-                turn(turned01[:, ft, P * c : P * (c + 1)], loss[c][:, P * ft : P * (ft + 1)], False, c == 1 and ft == 1)
         turned2 = psum.tile([P, 2, P], F32, name="turned2", tag="bank0")
         turned3 = psum.tile([P, 2, P], F32, name="turned3", tag="bank1")
-        for acc, c in ((turned2, 2), (turned3, 3)):
+        target = [turned01[:, :, 0:P], turned01[:, :, P : 2 * P], turned2[:], turned3[:]]
+        for c in range(1, 4):
             for ft in range(2):
-                nc.tensor.transpose(acc[:, ft, :], loss[c][:, P * ft : P * (ft + 1)], identity[:])
-        nc.scalar.activation(out=result01[:], in_=turned01[:], func=ACT.Relu)
-        nc.sync.dma_start(out=rows_out[:, :, 0 : 2 * P], in_=result01[:])
-        nc.scalar.activation(out=result2[:], in_=turned2[:], func=ACT.Relu)
+                turn(target[c][:, ft, :], loss[c][:, P * ft : P * (ft + 1)], c > 1 and ft == 0, False)
+        for ft in range(2):
+            turn(target[1][:, ft, :], far[:, 0, P * ft : P * (ft + 1)], False, False)
+        for ft in range(2):
+            turn(target[2][:, ft, :], far[:, 1, P * ft : P * (ft + 1)], False, ft == 1)
+        for ft in range(2):
+            turn(target[0][:, ft, :], loss[0][:, P * ft : P * (ft + 1)], False, ft == 1)
+        for ft in range(2):
+            turn(target[3][:, ft, :], far[:, 2, P * ft : P * (ft + 1)], False, ft == 1)
+        nc.scalar.activation(out=result2[:], in_=turned2[:], func=ACT.Relu, scale=-1.0)
         nc.scalar.dma_start(out=rows_out[:, :, 2 * P : 3 * P], in_=result2[:])
-        nc.vector.tensor_scalar(out=result3[:], in0=turned3[:], scalar1=0.0, scalar2=None, op0=ALU.max)
-        nc.sync.dma_start(out=rows_out[:, :, 3 * P : 4 * P], in_=result3[:])
+        nc.vector.tensor_scalar(out=result01[:], in0=turned01[:], scalar1=-1.0, scalar2=0.0, op0=ALU.mult, op1=ALU.max)
+        nc.sync.dma_start(out=rows_out[:, :, 0 : 2 * P], in_=result01[:])
+        nc.scalar.activation(out=result3[:], in_=turned3[:], func=ACT.Relu, scale=-1.0)
+        nc.scalar.dma_start(out=rows_out[:, :, 3 * P : 4 * P], in_=result3[:])

@@ -40,7 +40,7 @@ def tile_picked_triplet_none_e_kernel(tc, xT, w1_words, w1_scales, margin, offs,
         planes = [keep.tile([P, T], F32, name=f"plane{j}") for j in range(PACK)]
         rounded = [keep.tile([P, T], BF16, name=f"rounded{j}") for j in range(PACK)]
         picked = [keep.tile([P, V, PACK], BF16, name=f"picked{i}", align_bytes=64) for i in range(3)]
-        words = keep.tile([P, 8 * P], U32, name="words", align_bytes=64)
+        words = keep.tile([P, 9 * P], U32, name="words", align_bytes=64)
         scale_bytes = keep.tile([P, S], U8, name="scale_bytes", align_bytes=64)
 
         nc.vector.memset(w_scales[:].bitcast(I32), 0)
@@ -78,10 +78,10 @@ def tile_picked_triplet_none_e_kernel(tc, xT, w1_words, w1_scales, margin, offs,
             for i, sign in ((ANCHOR, -1.0), (NEGATIVE, 1.0)):
                 nc.scalar.activation(out=picked[i][:, :, j], in_=rounded[j][:].indirect(third(i)), func=ACT.Copy, scale=sign)
 
-        first_chunk = {(POSITIVE, 0): 0, (POSITIVE, 1): 2, (ANCHOR, 0): 5, (ANCHOR, 1): 0, (NEGATIVE, 0): 4, (NEGATIVE, 1): 2}
+        word_chunk = {POSITIVE: (2, 3, 0, 1), ANCHOR: (0, 1, 4, 5), NEGATIVE: (6, 7, 4, 8)}
 
         def place(i, v):
-            return P * first_chunk[i, v // (V // 2)] + v % (V // 2)
+            return P * word_chunk[i][v // P] + v % P
 
         def quantise(i, v0=0, v1=V):
             nc.vector.quantize_mx(
@@ -105,85 +105,90 @@ def tile_picked_triplet_none_e_kernel(tc, xT, w1_words, w1_scales, margin, offs,
             nc.tensor.matmul(out=acc, lhsT=src, rhs=identity[:], start=start, stop=stop, is_transpose=True)
 
         H = V // 2
-        alone = [psum.tile([P, N], F32, name=f"alone{i}", tag=f"bank{i}") for i in range(3)]
-        pos1 = psum.tile([P, N], F32, name="pos1")
-        pos23 = psum.tile([P, 2, N], F32, name="pos23")
+        LONE = 2
+        alone = {i: psum.tile([P, N], F32, name=f"alone{i}", tag=f"bank{i}") for i in (ANCHOR, POSITIVE)}
+        pos3 = psum.tile([P, N], F32, name="pos3", tag="bank3")
+        pos01 = psum.tile([P, 2, N], F32, name="pos01", tag="bank2")
+        neg0 = psum.tile([P, N], F32, name="neg0")
         neg1 = psum.tile([P, N], F32, name="neg1")
-        neg23 = psum.tile([P, 2, N], F32, name="neg23")
-        turned01 = psum.tile([P, 2, 2 * P], F32, name="turned01")
+        late = [psum.tile([P, H], F32, name=f"late{ft}") for ft in range(2)]
         positives = keep.tile([P, N], F32, name="positives")
         partial = keep.tile([P, N], F32, name="partial")
         apart = keep.tile([P, N], F32, name="apart")
         summed = keep.tile([P, N], F32, name="summed")
-        near = keep.tile([P, 3, N], F32, name="near")
-        far = keep.tile([P, 3, N], F32, name="far")
-        loss = [keep.tile([P, N], F32, name=f"loss{c}") for c in range(4)]
-        result01 = keep.tile([P, 2, 2 * P], F32, name="result01")
-        result2 = keep.tile([P, 2, P], F32, name="result2")
-        result3 = keep.tile([P, 2, P], F32, name="result3")
+        product = keep.tile([P, N], F32, name="product")
+        near = keep.tile([P, 4, N], F32, name="near")
+        minus_near = keep.tile([P, 4, N], F32, name="minus_near")
+        far = keep.tile([P, 4, N], F32, name="far")
+        result_early = [keep.tile([P, H], F32, name=f"result_early{ft}") for ft in range(2)]
+        result_late = [keep.tile([P, H], F32, name=f"result_late{ft}") for ft in range(2)]
 
-        minus_margin = keep.tile([P, 1], F32, name="minus_margin")
-        nc.gpsimd.tensor_scalar(out=minus_margin[:], in0=margins[:, 0:1], scalar1=-1.0, scalar2=0.0, op0=ALU.mult, op1=ALU.add)
+        minus_margin = keep.tile([P, 4], F32, name="minus_margin")
+        nc.gpsimd.tensor_scalar(out=minus_margin[:], in0=margins[:], scalar1=-1.0, scalar2=0.0, op0=ALU.mult, op1=ALU.add)
         for ft in range(2):
-            turn(turned01[:, ft, 0:P], minus_margin[:, 0:1].to_broadcast([P, P]), ft == 0, False)
+            turn(late[ft][:, 0:P], minus_margin[:, LONE : LONE + 1].to_broadcast([P, P]), True, False)
 
-        quantise(POSITIVE, 0, H)
         quantise(POSITIVE, H, V)
-        project(alone[POSITIVE][:], POSITIVE, 0, True, True)
-        project(pos1[:], POSITIVE, 1, True, False)
-        project(pos23[:, 0, :], POSITIVE, 2, True, False)
+        quantise(POSITIVE, 0, H)
+        project(alone[POSITIVE][:], POSITIVE, LONE, True, True)
+        project(pos3[:], POSITIVE, 3, True, False)
+        project(pos01[:, 0, :], POSITIVE, 0, True, False)
         nc.vector.tensor_copy(out=positives[:], in_=alone[POSITIVE][:])
-        quantise(ANCHOR, 0, H)
-        project(alone[ANCHOR][:], ANCHOR, 0, True, True)
-        project(pos1[:], ANCHOR, 1, False, True)
-        project(pos23[:, 1, :], POSITIVE, 3, False, False)
         quantise(ANCHOR, H, V)
-        project(pos23[:, 0, :], ANCHOR, 2, False, False)
-        project(pos23[:, 1, :], ANCHOR, 3, False, True)
+        project(alone[ANCHOR][:], ANCHOR, LONE, True, True)
+        project(pos3[:], ANCHOR, 3, False, True)
+        project(pos01[:, 1, :], POSITIVE, 1, False, False)
+        quantise(ANCHOR, 0, H)
+        project(pos01[:, 0, :], ANCHOR, 0, False, False)
+        project(pos01[:, 1, :], ANCHOR, 1, False, True)
+        project(neg0[:], ANCHOR, 0, True, False)
         project(neg1[:], ANCHOR, 1, True, False)
-        project(neg23[:, 0, :], ANCHOR, 2, True, False)
-        project(neg23[:, 1, :], ANCHOR, 3, False, False)
         nc.vector.scalar_tensor_tensor(
             out=partial[:], in0=alone[ANCHOR][:], scalar=2.0, in1=positives[:], op0=ALU.mult, op1=ALU.add
         )
+        quantise(NEGATIVE, LONE * P, (LONE + 1) * P)
         quantise(NEGATIVE, 0, H)
-        quantise(NEGATIVE, H, V)
-        project(alone[NEGATIVE][:], NEGATIVE, 0, True, True)
+        quantise(NEGATIVE, 3 * P, V)
+        alone[NEGATIVE] = psum.tile([P, N], F32, name="alone_negative", tag=f"bank{ANCHOR}")
+        project(alone[NEGATIVE][:], NEGATIVE, LONE, True, True)
+        project(neg0[:], NEGATIVE, 0, False, True)
         project(neg1[:], NEGATIVE, 1, False, True)
-        project(neg23[:, 0, :], NEGATIVE, 2, False, False)
-        project(neg23[:, 1, :], NEGATIVE, 3, False, True)
 
-        nc.scalar.activation(out=near[:, 0, :], in_=pos1[:], func=ACT.Square)
-        nc.scalar.activation(out=near[:, 1:3, :], in_=pos23[:], func=ACT.Square)
-        nc.scalar.activation(out=far[:, 0, :], in_=neg1[:], func=ACT.Square)
-        nc.scalar.activation(out=far[:, 1, :], in_=neg23[:, 0, :], func=ACT.Square)
-        nc.scalar.activation(out=far[:, 2, :], in_=neg23[:, 1, :], func=ACT.Square)
+        nc.scalar.activation(out=near[:, 3, :], in_=pos3[:], func=ACT.Square)
+        nc.scalar.activation(out=near[:, 0:2, :], in_=pos01[:], func=ACT.Square)
+        for c in (3,):
+            nc.scalar.activation(
+                out=minus_near[:, c, :], in_=near[:, c, :], func=ACT.Identity, scale=-1.0, bias=minus_margin[:, c : c + 1]
+            )
+        neg3 = psum.tile([P, N], F32, name="neg3", tag="bank2")
+        project(neg3[:], ANCHOR, 3, True, False)
+        project(neg3[:], NEGATIVE, 3, False, True)
+        for c, acc in ((0, neg0), (1, neg1), (3, neg3)):
+            nc.scalar.activation(out=far[:, c, :], in_=acc[:], func=ACT.Square)
 
-        for c in range(1, 4):
+        for c in (0, 1):
             nc.vector.tensor_scalar(
-                out=loss[c][:], in0=near[:, c - 1, :], scalar1=margins[:, c : c + 1], scalar2=-1.0, op0=ALU.add, op1=ALU.mult
+                out=minus_near[:, c, :], in0=near[:, c, :], scalar1=margins[:, c : c + 1], scalar2=-1.0, op0=ALU.add, op1=ALU.mult
             )
         nc.vector.tensor_tensor(out=apart[:], in0=alone[NEGATIVE][:], in1=positives[:], op=ALU.subtract)
         nc.vector.tensor_tensor(out=summed[:], in0=alone[NEGATIVE][:], in1=partial[:], op=ALU.add)
-        nc.vector.tensor_tensor(out=loss[0][:], in0=apart[:], in1=summed[:], op=ALU.mult)
-        rows_out = out.rearrange("(f p) v -> p f v", p=P)
-        turned2 = psum.tile([P, 2, P], F32, name="turned2", tag="bank0")
-        turned3 = psum.tile([P, 2, P], F32, name="turned3", tag="bank1")
-        target = [turned01[:, :, 0:P], turned01[:, :, P : 2 * P], turned2[:], turned3[:]]
-        for c in range(1, 4):
-            for ft in range(2):
-                turn(target[c][:, ft, :], loss[c][:, P * ft : P * (ft + 1)], c > 1 and ft == 0, False)
+        nc.vector.tensor_tensor(out=product[:], in0=apart[:], in1=summed[:], op=ALU.mult)
+
+        early = [psum.tile([P, H], F32, name=f"early{ft}", tag=tag) for ft, tag in enumerate((f"bank{POSITIVE}", "bank3"))]
+        for src in (minus_near, far):
+            for c in (0, 1):
+                for ft in range(2):
+                    first = src is minus_near and c == 0
+                    last = src is far and c == 1
+                    turn(early[ft][:, P * c : P * (c + 1)], src[:, c, P * ft : P * (ft + 1)], first, last)
         for ft in range(2):
-            turn(target[1][:, ft, :], far[:, 0, P * ft : P * (ft + 1)], False, False)
+            turn(late[ft][:, P : 2 * P], minus_near[:, 3, P * ft : P * (ft + 1)], False, False)
         for ft in range(2):
-            turn(target[2][:, ft, :], far[:, 1, P * ft : P * (ft + 1)], False, ft == 1)
+            turn(late[ft][:, P : 2 * P], far[:, 3, P * ft : P * (ft + 1)], False, False)
         for ft in range(2):
-            turn(target[0][:, ft, :], loss[0][:, P * ft : P * (ft + 1)], False, ft == 1)
-        for ft in range(2):
-            turn(target[3][:, ft, :], far[:, 2, P * ft : P * (ft + 1)], False, ft == 1)
-        nc.scalar.activation(out=result2[:], in_=turned2[:], func=ACT.Relu, scale=-1.0)
-        nc.scalar.dma_start(out=rows_out[:, :, 2 * P : 3 * P], in_=result2[:])
-        nc.vector.tensor_scalar(out=result01[:], in0=turned01[:], scalar1=-1.0, scalar2=0.0, op0=ALU.mult, op1=ALU.max)
-        nc.sync.dma_start(out=rows_out[:, :, 0 : 2 * P], in_=result01[:])
-        nc.scalar.activation(out=result3[:], in_=turned3[:], func=ACT.Relu, scale=-1.0)
-        nc.scalar.dma_start(out=rows_out[:, :, 3 * P : 4 * P], in_=result3[:])
+            turn(late[ft][:, 0:P], product[:, P * ft : P * (ft + 1)], False, True)
+        for acc, res, cols in ((early, result_early, slice(0, H)), (late, result_late, slice(H, V))):
+            nc.vector.tensor_scalar(out=res[0][:], in0=acc[0][:], scalar1=-1.0, scalar2=0.0, op0=ALU.mult, op1=ALU.max)
+            nc.sync.dma_start(out=out[0:P, cols], in_=res[0][:])
+            nc.scalar.activation(out=res[1][:], in_=acc[1][:], func=ACT.Relu, scale=-1.0)
+            (nc.sync if acc is early else nc.scalar).dma_start(out=out[P : 2 * P, cols], in_=res[1][:])

@@ -40,10 +40,14 @@ def tile_picked_triplet_none_e_kernel(tc, xT, w1_words, w1_scales, margin, offs,
         planes = [keep.tile([P, T], F32, name=f"plane{j}") for j in range(PACK)]
         rounded = [keep.tile([P, T], BF16, name=f"rounded{j}") for j in range(PACK)]
         picked = [keep.tile([P, V, PACK], BF16, name=f"picked{i}", align_bytes=64) for i in range(3)]
-        words = keep.tile([P, 9 * P], U32, name="words", align_bytes=64)
-        scale_bytes = keep.tile([P, S], U8, name="scale_bytes", align_bytes=64)
+        words = keep.tile([P, 10 * P], U32, name="words", align_bytes=64)
+        scale_bytes = keep.tile([P, 2 * V], U8, name="scale_bytes", align_bytes=64)
+        two = keep.tile([P, 1], F32, name="two", tag="late", align_bytes=64)
+        nc.vector.memset(two[:], 2.0)
 
         nc.vector.memset(w_scales[:].bitcast(I32), 0)
+        margin_row = keep.tile([P, V], F32, name="margin_row")
+        nc.vector.memset(margin_row[:], 0.0)
         rows = xT.rearrange("(p j) t -> j p t", j=PACK)
         for j in range(PACK):
             c0 = 0
@@ -51,6 +55,7 @@ def tile_picked_triplet_none_e_kernel(tc, xT, w1_words, w1_scales, margin, offs,
                 nc.sync.dma_start(out=planes[j][:, c0 : c0 + width], in_=rows[j][:, c0 : c0 + width])
                 if j == 0 and c0 == 0:
                     nc.sync.dma_start(offsets[:], offs)
+                    nc.sync.dma_start(out=margin_row[0:1, :], in_=margin[0:1, :])
                 c0 = c0 + width
             if j == 0:
                 for q in range(P // 32):
@@ -58,8 +63,6 @@ def tile_picked_triplet_none_e_kernel(tc, xT, w1_words, w1_scales, margin, offs,
                         out=w_scales[32 * q : 32 * q + 4, :].bitcast(I32),
                         in_=w1_scales[0, 4 * q : 4 * q + 4, :].bitcast(I32),
                     )
-        with nc.allow_non_contiguous_dma(reason="one margin to a partition"):
-            nc.sync.dma_start(out=margins[:], in_=margin[0].rearrange("(c p) -> p c", p=P))
         nc.sync.dma_start(out=w_words[:].bitcast(I32), in_=w1_words[0].rearrange("p n t -> p (n t)").bitcast(I32))
 
         def third(i):
@@ -78,15 +81,17 @@ def tile_picked_triplet_none_e_kernel(tc, xT, w1_words, w1_scales, margin, offs,
             for i, sign in ((ANCHOR, -1.0), (NEGATIVE, 1.0)):
                 nc.scalar.activation(out=picked[i][:, :, j], in_=rounded[j][:].indirect(third(i)), func=ACT.Copy, scale=sign)
 
-        word_chunk = {POSITIVE: (2, 3, 0, 1), ANCHOR: (0, 1, 4, 5), NEGATIVE: (6, 7, 4, 8)}
+        word_chunk = {POSITIVE: (2, 3, 0, 1), ANCHOR: (0, 1, 4, 5), NEGATIVE: (6, 7, 9, 8)}
 
         def place(i, v):
             return P * word_chunk[i][v // P] + v % P
 
+        scales = {i: scale_bytes[:, i * V : (i + 1) * V] for i in (ANCHOR, POSITIVE)}
+
         def quantise(i, v0=0, v1=V):
             nc.vector.quantize_mx(
                 out=words[:, place(i, v0) : place(i, v0) + v1 - v0].bitcast(FP8X4),
-                scales=scale_bytes[:, i * V + v0 : i * V + v1],
+                scales=scales[i][:, v0:v1],
                 in_=picked[i][:, v0:v1, :].rearrange("p v j -> p (v j)"),
             )
 
@@ -94,7 +99,7 @@ def tile_picked_triplet_none_e_kernel(tc, xT, w1_words, w1_scales, margin, offs,
             nc.tensor.matmul_mx(
                 out=acc,
                 lhsT=words[:, place(i, P * c) : place(i, P * c) + P].bitcast(FP8X4),
-                lhsT_scale=scale_bytes[:, i * V + P * c : i * V + P * (c + 1)],
+                lhsT_scale=scales[i][:, P * c : P * (c + 1)],
                 rhs=w_words[:].bitcast(FP8X4),
                 rhs_scale=w_scales[:],
                 start=start,
@@ -110,9 +115,8 @@ def tile_picked_triplet_none_e_kernel(tc, xT, w1_words, w1_scales, margin, offs,
         pos3 = psum.tile([P, N], F32, name="pos3", tag="bank3")
         pos01 = psum.tile([P, 2, N], F32, name="pos01", tag="bank2")
         neg0 = psum.tile([P, N], F32, name="neg0")
-        neg1 = psum.tile([P, N], F32, name="neg1")
         late = [psum.tile([P, H], F32, name=f"late{ft}") for ft in range(2)]
-        positives = keep.tile([P, N], F32, name="positives")
+        positives = picked[ANCHOR][:, H:V, :].rearrange("p v j -> p (v j)").bitcast(F32)[:, 0:N]
         partial = keep.tile([P, N], F32, name="partial")
         apart = keep.tile([P, N], F32, name="apart")
         summed = keep.tile([P, N], F32, name="summed")
@@ -124,17 +128,23 @@ def tile_picked_triplet_none_e_kernel(tc, xT, w1_words, w1_scales, margin, offs,
         result_late = [keep.tile([P, H], F32, name=f"result_late{ft}") for ft in range(2)]
 
         minus_margin = keep.tile([P, 4], F32, name="minus_margin")
-        nc.gpsimd.tensor_scalar(out=minus_margin[:], in0=margins[:], scalar1=-1.0, scalar2=0.0, op0=ALU.mult, op1=ALU.add)
+        turned_row = psum.tile([P, 4, P], F32, name="turned_row", tag="bank4")
+        for c in range(4):
+            nc.tensor.transpose(turned_row[:, c, :], margin_row[:, P * c : P * (c + 1)], identity[:])
+        nc.scalar.activation(out=margins[:], in_=turned_row[:, :, 0], func=ACT.Copy)
+        nc.scalar.activation(out=minus_margin[:], in_=turned_row[:, :, 0], func=ACT.Copy, scale=-1.0)
         for ft in range(2):
             turn(late[ft][:, 0:P], minus_margin[:, LONE : LONE + 1].to_broadcast([P, P]), True, False)
 
-        quantise(POSITIVE, H, V)
+        neg3 = psum.tile([P, N], F32, name="neg3", tag="bank4")
+        quantise(POSITIVE, H, H + P)
+        quantise(POSITIVE, H + P, V)
         quantise(POSITIVE, 0, H)
         project(alone[POSITIVE][:], POSITIVE, LONE, True, True)
         project(pos3[:], POSITIVE, 3, True, False)
         project(pos01[:, 0, :], POSITIVE, 0, True, False)
-        nc.vector.tensor_copy(out=positives[:], in_=alone[POSITIVE][:])
         quantise(ANCHOR, H, V)
+        nc.vector.tensor_copy(out=positives, in_=alone[POSITIVE][:])
         project(alone[ANCHOR][:], ANCHOR, LONE, True, True)
         project(pos3[:], ANCHOR, 3, False, True)
         project(pos01[:, 1, :], POSITIVE, 1, False, False)
@@ -142,10 +152,13 @@ def tile_picked_triplet_none_e_kernel(tc, xT, w1_words, w1_scales, margin, offs,
         project(pos01[:, 0, :], ANCHOR, 0, False, False)
         project(pos01[:, 1, :], ANCHOR, 1, False, True)
         project(neg0[:], ANCHOR, 0, True, False)
+        neg1 = psum.tile([P, N], F32, name="neg1", tag=f"bank{POSITIVE}")
         project(neg1[:], ANCHOR, 1, True, False)
         nc.vector.scalar_tensor_tensor(
-            out=partial[:], in0=alone[ANCHOR][:], scalar=2.0, in1=positives[:], op0=ALU.mult, op1=ALU.add
+            out=partial[:], in0=alone[ANCHOR][:], scalar=two[:, 0:1], in1=positives, op0=ALU.mult, op1=ALU.add
         )
+        late_scales = keep.tile([P, V], U8, name="late_scales", tag="late", align_bytes=64)
+        scales[NEGATIVE] = late_scales[:]
         quantise(NEGATIVE, LONE * P, (LONE + 1) * P)
         quantise(NEGATIVE, 0, H)
         quantise(NEGATIVE, 3 * P, V)
@@ -153,6 +166,8 @@ def tile_picked_triplet_none_e_kernel(tc, xT, w1_words, w1_scales, margin, offs,
         project(alone[NEGATIVE][:], NEGATIVE, LONE, True, True)
         project(neg0[:], NEGATIVE, 0, False, True)
         project(neg1[:], NEGATIVE, 1, False, True)
+        project(neg3[:], NEGATIVE, 3, True, False)
+        project(neg3[:], ANCHOR, 3, False, True)
 
         nc.scalar.activation(out=near[:, 3, :], in_=pos3[:], func=ACT.Square)
         nc.scalar.activation(out=near[:, 0:2, :], in_=pos01[:], func=ACT.Square)
@@ -160,9 +175,6 @@ def tile_picked_triplet_none_e_kernel(tc, xT, w1_words, w1_scales, margin, offs,
             nc.scalar.activation(
                 out=minus_near[:, c, :], in_=near[:, c, :], func=ACT.Identity, scale=-1.0, bias=minus_margin[:, c : c + 1]
             )
-        neg3 = psum.tile([P, N], F32, name="neg3", tag="bank2")
-        project(neg3[:], ANCHOR, 3, True, False)
-        project(neg3[:], NEGATIVE, 3, False, True)
         for c, acc in ((0, neg0), (1, neg1), (3, neg3)):
             nc.scalar.activation(out=far[:, c, :], in_=acc[:], func=ACT.Square)
 
@@ -170,11 +182,11 @@ def tile_picked_triplet_none_e_kernel(tc, xT, w1_words, w1_scales, margin, offs,
             nc.vector.tensor_scalar(
                 out=minus_near[:, c, :], in0=near[:, c, :], scalar1=margins[:, c : c + 1], scalar2=-1.0, op0=ALU.add, op1=ALU.mult
             )
-        nc.vector.tensor_tensor(out=apart[:], in0=alone[NEGATIVE][:], in1=positives[:], op=ALU.subtract)
+        nc.vector.tensor_tensor(out=apart[:], in0=alone[NEGATIVE][:], in1=positives, op=ALU.subtract)
         nc.vector.tensor_tensor(out=summed[:], in0=alone[NEGATIVE][:], in1=partial[:], op=ALU.add)
         nc.vector.tensor_tensor(out=product[:], in0=apart[:], in1=summed[:], op=ALU.mult)
 
-        early = [psum.tile([P, H], F32, name=f"early{ft}", tag=tag) for ft, tag in enumerate((f"bank{POSITIVE}", "bank3"))]
+        early = [psum.tile([P, H], F32, name=f"early{ft}", tag=tag) for ft, tag in enumerate(("bank2", "bank3"))]
         for src in (minus_near, far):
             for c in (0, 1):
                 for ft in range(2):

@@ -20,7 +20,7 @@ FP8X4 = mybir.dt.float8_e4m3fn_x4
 ACT = mybir.ActivationFunctionType
 ALU = mybir.AluOpType
 
-CHUNKS = [[2048, 2048], [2048, 1024, 1024], [2048, 1024, 512, 512], [2048, 1024, 512, 256, 256]]
+CHUNKS = [[4096], [2048, 2048], [2560, 1536], [2048, 1024, 768, 256]]
 LAST_CAST_ON_VECTOR = 320
 MARGIN_ON_GPSIMD = 256
 
@@ -72,7 +72,10 @@ def tile_picked_triplet_none_e_kernel(tc, xT, w1_words, w1_scales, margin, offs,
             c0 = 0
             for width in CHUNKS[j]:
                 c1 = c0 + width
-                if (j == 0 and c0 == 0) or (j == PACK - 1 and c1 == T):
+                if j == 0:
+                    nc.scalar.activation(out=rounded[j][:, 0:1408], in_=planes[j][:, 0:1408], func=ACT.Copy)
+                    nc.vector.tensor_copy(out=rounded[j][:, 1408:T], in_=planes[j][:, 1408:T])
+                elif j == PACK - 1 and c1 == T:
                     nc.scalar.activation(out=rounded[j][:, c0:c1], in_=planes[j][:, c0:c1], func=ACT.Copy)
                 else:
                     nc.vector.tensor_copy(out=rounded[j][:, c0:c1], in_=planes[j][:, c0:c1])

@@ -21,8 +21,7 @@ ACT = mybir.ActivationFunctionType
 ALU = mybir.AluOpType
 
 CHUNKS = [[4096], [2048, 2048], [2560, 1536], [2048, 1024, 768, 256]]
-LAST_CAST_ON_VECTOR = 320
-MARGIN_ON_GPSIMD = 256
+ROUNDED_BY_SCALAR = [[1408], [0, 0], [0, 384], [0, 0, 0, 256]]
 
 
 def tile_picked_triplet_none_e_kernel(tc, xT, w1_words, w1_scales, margin, offs, out):
@@ -34,7 +33,6 @@ def tile_picked_triplet_none_e_kernel(tc, xT, w1_words, w1_scales, margin, offs,
         offsets = keep.tile([P, S // LIST_ROWS], U16, name="offsets")
         w_words = keep.tile([P, N], U32, name="w_words", align_bytes=64)
         w_scales = keep.tile([P, N], U8, name="w_scales", align_bytes=64)
-        margins = keep.tile([P, V // P], F32, name="margins")
         identity = keep.tile([P, P], F32, name="identity")
         make_identity(nc, identity[:])
         planes = [keep.tile([P, T], F32, name=f"plane{j}") for j in range(PACK)]
@@ -70,15 +68,12 @@ def tile_picked_triplet_none_e_kernel(tc, xT, w1_words, w1_scales, margin, offs,
 
         for j in range(PACK):
             c0 = 0
-            for width in CHUNKS[j]:
-                c1 = c0 + width
-                if j == 0:
-                    nc.scalar.activation(out=rounded[j][:, 0:1408], in_=planes[j][:, 0:1408], func=ACT.Copy)
-                    nc.vector.tensor_copy(out=rounded[j][:, 1408:T], in_=planes[j][:, 1408:T])
-                elif j == PACK - 1 and c1 == T:
-                    nc.scalar.activation(out=rounded[j][:, c0:c1], in_=planes[j][:, c0:c1], func=ACT.Copy)
-                else:
-                    nc.vector.tensor_copy(out=rounded[j][:, c0:c1], in_=planes[j][:, c0:c1])
+            for width, on_scalar in zip(CHUNKS[j], ROUNDED_BY_SCALAR[j]):
+                mid, c1 = c0 + on_scalar, c0 + width
+                if mid > c0:
+                    nc.scalar.activation(out=rounded[j][:, c0:mid], in_=planes[j][:, c0:mid], func=ACT.Copy)
+                if c1 > mid:
+                    nc.vector.tensor_copy(out=rounded[j][:, mid:c1], in_=planes[j][:, mid:c1])
                 c0 = c1
             nc.vector.tensor_copy(out=picked[POSITIVE][:, :, j], in_=planes[j][:].indirect(third(POSITIVE)))
             for i, sign in ((ANCHOR, -1.0), (NEGATIVE, 1.0)):
@@ -134,7 +129,6 @@ def tile_picked_triplet_none_e_kernel(tc, xT, w1_words, w1_scales, margin, offs,
         turned_row = psum.tile([P, 4, P], F32, name="turned_row", tag="bank4")
         for c in range(4):
             nc.tensor.transpose(turned_row[:, c, :], margin_row[:, P * c : P * (c + 1)], identity[:])
-        nc.scalar.activation(out=margins[:], in_=turned_row[:, :, 0], func=ACT.Copy)
         nc.scalar.activation(out=minus_margin[:], in_=turned_row[:, :, 0], func=ACT.Copy, scale=-1.0)
         for ft in range(2):
             turn(late[ft][:, 0:P], minus_margin[:, LONE : LONE + 1].to_broadcast([P, P]), True, False)
@@ -183,7 +177,7 @@ def tile_picked_triplet_none_e_kernel(tc, xT, w1_words, w1_scales, margin, offs,
 
         for c in (0, 1):
             nc.vector.tensor_scalar(
-                out=minus_near[:, c, :], in0=near[:, c, :], scalar1=margins[:, c : c + 1], scalar2=-1.0, op0=ALU.add, op1=ALU.mult
+                out=minus_near[:, c, :], in0=near[:, c, :], scalar1=-1.0, scalar2=minus_margin[:, c : c + 1], op0=ALU.mult, op1=ALU.add
             )
         nc.vector.tensor_tensor(out=apart[:], in0=alone[NEGATIVE][:], in1=positives, op=ALU.subtract)
         nc.vector.tensor_tensor(out=summed[:], in0=alone[NEGATIVE][:], in1=partial[:], op=ALU.add)

@@ -20,8 +20,8 @@ FP8X4 = mybir.dt.float8_e4m3fn_x4
 ACT = mybir.ActivationFunctionType
 ALU = mybir.AluOpType
 
-CHUNKS = [[4096], [2048, 2048], [2560, 1536], [2048, 1024, 768, 256]]
-ROUNDED_BY_SCALAR = [[1408], [0, 0], [0, 384], [0, 0, 0, 256]]
+CHUNKS = [[4096], [2048, 2048], [2560, 1536], [2048, 1152, 512, 384]]
+ROUNDED_BY_SCALAR = [[1408], [0, 0], [0, 384], [0, 0, 0, 384]]
 
 
 def tile_picked_triplet_none_e_kernel(tc, xT, w1_words, w1_scales, margin, offs, out):

@@ -8,6 +8,8 @@ P = 128
 PACK = 4
 LIST_ROWS = 16
 ANCHOR, POSITIVE, NEGATIVE = 0, 1, 2
+H = V // 2
+LONE = 2
 FLOPS = 2 * K * N * S
 
 F32 = mybir.dt.float32
@@ -19,9 +21,6 @@ U8 = mybir.dt.uint8
 FP8X4 = mybir.dt.float8_e4m3fn_x4
 ACT = mybir.ActivationFunctionType
 ALU = mybir.AluOpType
-
-CHUNKS = [[4096], [2048, 2048], [2560, 1536], [2048, 1152, 512, 384]]
-ROUNDED_BY_SCALAR = [[1408], [0, 0], [0, 384], [0, 0, 0, 384]]
 
 
 def tile_picked_triplet_none_e_kernel(tc, xT, w1_words, w1_scales, margin, offs, out):
@@ -36,26 +35,20 @@ def tile_picked_triplet_none_e_kernel(tc, xT, w1_words, w1_scales, margin, offs,
         identity = keep.tile([P, P], F32, name="identity")
         make_identity(nc, identity[:])
         planes = [keep.tile([P, T], F32, name=f"plane{j}") for j in range(PACK)]
-        rounded = [keep.tile([P, T], BF16, name=f"rounded{j}") for j in range(PACK)]
+        dense = [keep.tile([P, 2 * V], BF16, name=f"dense{j}") for j in range(PACK)]
         picked = [keep.tile([P, V, PACK], BF16, name=f"picked{i}", align_bytes=64) for i in range(3)]
-        words = keep.tile([P, 10 * P], U32, name="words", align_bytes=64)
-        scale_bytes = keep.tile([P, 2 * V], U8, name="scale_bytes", align_bytes=64)
-        two = keep.tile([P, 1], F32, name="two", tag="late", align_bytes=64)
-        nc.vector.memset(two[:], 2.0)
+        words = [keep.tile([P, V], U32, name=f"words{i}", align_bytes=64) for i in range(3)]
+        scales = [keep.tile([P, V], U8, name=f"scales{i}", align_bytes=64) for i in range(3)]
 
         nc.vector.memset(w_scales[:].bitcast(I32), 0)
         margin_row = keep.tile([P, V], F32, name="margin_row")
         nc.vector.memset(margin_row[:], 0.0)
         rows = xT.rearrange("(p j) t -> j p t", j=PACK)
         for j in range(PACK):
-            c0 = 0
-            for width in CHUNKS[j]:
-                nc.sync.dma_start(out=planes[j][:, c0 : c0 + width], in_=rows[j][:, c0 : c0 + width])
-                if j == 0 and c0 == 0:
-                    nc.sync.dma_start(offsets[:], offs)
-                    nc.sync.dma_start(out=margin_row[0:1, :], in_=margin[0:1, :])
-                c0 = c0 + width
+            nc.sync.dma_start(out=planes[j][:], in_=rows[j])
             if j == 0:
+                nc.sync.dma_start(offsets[:], offs)
+                nc.sync.dma_start(out=margin_row[0:1, :], in_=margin[0:1, :])
                 for q in range(P // 32):
                     nc.sync.dma_start(
                         out=w_scales[32 * q : 32 * q + 4, :].bitcast(I32),
@@ -63,32 +56,29 @@ def tile_picked_triplet_none_e_kernel(tc, xT, w1_words, w1_scales, margin, offs,
                     )
         nc.sync.dma_start(out=w_words[:].bitcast(I32), in_=w1_words[0].rearrange("p n t -> p (n t)").bitcast(I32))
 
-        def third(i):
-            return offsets[:, i * V // LIST_ROWS : (i + 1) * V // LIST_ROWS]
+        def entries(s0, s1):
+            return offsets[:, s0 // LIST_ROWS : s1 // LIST_ROWS]
 
         for j in range(PACK):
-            c0 = 0
-            for width, on_scalar in zip(CHUNKS[j], ROUNDED_BY_SCALAR[j]):
-                mid, c1 = c0 + on_scalar, c0 + width
-                if mid > c0:
-                    nc.scalar.activation(out=rounded[j][:, c0:mid], in_=planes[j][:, c0:mid], func=ACT.Copy)
-                if c1 > mid:
-                    nc.vector.tensor_copy(out=rounded[j][:, mid:c1], in_=planes[j][:, mid:c1])
-                c0 = c1
-            nc.vector.tensor_copy(out=picked[POSITIVE][:, :, j], in_=planes[j][:].indirect(third(POSITIVE)))
-            for i, sign in ((ANCHOR, -1.0), (NEGATIVE, 1.0)):
-                nc.scalar.activation(out=picked[i][:, :, j], in_=rounded[j][:].indirect(third(i)), func=ACT.Copy, scale=sign)
+            nc.vector.tensor_copy(out=picked[ANCHOR][:, :, j], in_=planes[j][:].indirect(entries(0, V)))
+            last = j == PACK - 1
+            cuts = (0, V, V + H, 2 * V) if last else (0, 2 * V)
+            for c0, c1 in zip(cuts[:-1], cuts[1:]):
+                nc.scalar.activation(
+                    out=dense[j][:, c0:c1], in_=planes[j][:].indirect(entries(V + c0, V + c1)), func=ACT.Copy, scale=-1.0
+                )
+            halves = ((0, H), (H, V)) if last else ((0, V),)
+            for v0, v1 in halves:
+                nc.vector.tensor_copy(out=picked[POSITIVE][:, v0:v1, j], in_=dense[j][:, v0:v1])
+            for v0, v1 in halves:
+                if j < 2:
+                    nc.vector.tensor_copy(out=picked[NEGATIVE][:, v0:v1, j], in_=dense[j][:, V + v0 : V + v1])
+                else:
+                    nc.scalar.copy(out=picked[NEGATIVE][:, v0:v1, j], in_=dense[j][:, V + v0 : V + v1])
 
-        word_chunk = {POSITIVE: (2, 3, 0, 1), ANCHOR: (0, 1, 4, 5), NEGATIVE: (6, 7, 9, 8)}
-
-        def place(i, v):
-            return P * word_chunk[i][v // P] + v % P
-
-        scales = {i: scale_bytes[:, i * V : (i + 1) * V] for i in (ANCHOR, POSITIVE)}
-
-        def quantise(i, v0=0, v1=V):
+        def quantise(i, v0, v1):
             nc.vector.quantize_mx(
-                out=words[:, place(i, v0) : place(i, v0) + v1 - v0].bitcast(FP8X4),
+                out=words[i][:, v0:v1].bitcast(FP8X4),
                 scales=scales[i][:, v0:v1],
                 in_=picked[i][:, v0:v1, :].rearrange("p v j -> p (v j)"),
             )
@@ -96,7 +86,7 @@ def tile_picked_triplet_none_e_kernel(tc, xT, w1_words, w1_scales, margin, offs,
         def project(acc, i, c, start, stop):
             nc.tensor.matmul_mx(
                 out=acc,
-                lhsT=words[:, place(i, P * c) : place(i, P * c) + P].bitcast(FP8X4),
+                lhsT=words[i][:, P * c : P * (c + 1)].bitcast(FP8X4),
                 lhsT_scale=scales[i][:, P * c : P * (c + 1)],
                 rhs=w_words[:].bitcast(FP8X4),
                 rhs_scale=w_scales[:],
@@ -107,95 +97,82 @@ def tile_picked_triplet_none_e_kernel(tc, xT, w1_words, w1_scales, margin, offs,
         def turn(acc, src, start, stop):
             nc.tensor.matmul(out=acc, lhsT=src, rhs=identity[:], start=start, stop=stop, is_transpose=True)
 
-        H = V // 2
-        LONE = 2
-        alone = {i: psum.tile([P, N], F32, name=f"alone{i}", tag=f"bank{i}") for i in (ANCHOR, POSITIVE)}
-        pos3 = psum.tile([P, N], F32, name="pos3", tag="bank3")
-        pos01 = psum.tile([P, 2, N], F32, name="pos01", tag="bank2")
-        neg0 = psum.tile([P, N], F32, name="neg0")
+        minus_margin = keep.tile([P, 4], F32, name="minus_margin")
+        turned_row = psum.tile([P, 4, P], F32, name="turned_row", tag="bank4")
+        for c in range(4):
+            nc.tensor.transpose(turned_row[:, c, :], margin_row[:, P * c : P * (c + 1)], identity[:])
+        nc.scalar.activation(out=minus_margin[:], in_=turned_row[:, :, 0], func=ACT.Copy, scale=-1.0)
         late = [psum.tile([P, H], F32, name=f"late{ft}") for ft in range(2)]
-        positives = picked[ANCHOR][:, H:V, :].rearrange("p v j -> p (v j)").bitcast(F32)[:, 0:N]
-        partial = keep.tile([P, N], F32, name="partial")
-        apart = keep.tile([P, N], F32, name="apart")
-        summed = keep.tile([P, N], F32, name="summed")
-        product = keep.tile([P, N], F32, name="product")
+        for ft in range(2):
+            turn(late[ft][:, 0:P], minus_margin[:, LONE : LONE + 1].to_broadcast([P, P]), True, False)
+
+        pos01 = psum.tile([P, 2, N], F32, name="pos01", tag="bank0")
+        pos23 = psum.tile([P, 2, N], F32, name="pos23", tag="bank1")
+        neg01 = psum.tile([P, 2, N], F32, name="neg01", tag="bank2")
+        neg3 = psum.tile([P, N], F32, name="neg3", tag="bank4")
+        anchors = psum.tile([P, N], F32, name="anchors", tag="bank5")
+        anchors_sb = keep.tile([P, N], F32, name="anchors_sb")
+        lone_pos = keep.tile([P, N], F32, name="lone_pos")
+        lone_neg = keep.tile([P, N], F32, name="lone_neg")
         near = keep.tile([P, 4, N], F32, name="near")
         minus_near = keep.tile([P, 4, N], F32, name="minus_near")
         far = keep.tile([P, 4, N], F32, name="far")
         result_early = [keep.tile([P, H], F32, name=f"result_early{ft}") for ft in range(2)]
         result_late = [keep.tile([P, H], F32, name=f"result_late{ft}") for ft in range(2)]
 
-        minus_margin = keep.tile([P, 4], F32, name="minus_margin")
-        turned_row = psum.tile([P, 4, P], F32, name="turned_row", tag="bank4")
-        for c in range(4):
-            nc.tensor.transpose(turned_row[:, c, :], margin_row[:, P * c : P * (c + 1)], identity[:])
-        nc.scalar.activation(out=minus_margin[:], in_=turned_row[:, :, 0], func=ACT.Copy, scale=-1.0)
-        for ft in range(2):
-            turn(late[ft][:, 0:P], minus_margin[:, LONE : LONE + 1].to_broadcast([P, P]), True, False)
-
-        neg3 = psum.tile([P, N], F32, name="neg3", tag="bank4")
-        quantise(POSITIVE, H, H + P)
-        quantise(POSITIVE, H + P, V)
-        quantise(POSITIVE, 0, H)
-        project(alone[POSITIVE][:], POSITIVE, LONE, True, True)
-        project(pos3[:], POSITIVE, 3, True, False)
-        project(pos01[:, 0, :], POSITIVE, 0, True, False)
+        quantise(ANCHOR, 0, P)
+        quantise(ANCHOR, P, H)
         quantise(ANCHOR, H, V)
-        nc.vector.tensor_copy(out=positives, in_=alone[POSITIVE][:])
-        project(alone[ANCHOR][:], ANCHOR, LONE, True, True)
-        project(pos3[:], ANCHOR, 3, False, True)
-        project(pos01[:, 1, :], POSITIVE, 1, False, False)
-        quantise(ANCHOR, 0, H)
-        project(pos01[:, 0, :], ANCHOR, 0, False, False)
-        project(pos01[:, 1, :], ANCHOR, 1, False, True)
-        project(neg0[:], ANCHOR, 0, True, False)
-        neg1 = psum.tile([P, N], F32, name="neg1", tag=f"bank{POSITIVE}")
-        project(neg1[:], ANCHOR, 1, True, False)
-        nc.vector.scalar_tensor_tensor(
-            out=partial[:], in0=alone[ANCHOR][:], scalar=two[:, 0:1], in1=positives, op0=ALU.mult, op1=ALU.add
-        )
-        late_scales = keep.tile([P, V], U8, name="late_scales", tag="late", align_bytes=64)
-        scales[NEGATIVE] = late_scales[:]
-        quantise(NEGATIVE, LONE * P, (LONE + 1) * P)
+        project(pos01[:, 0, :], ANCHOR, 0, True, False)
+        project(neg01[:, 0, :], ANCHOR, 0, True, False)
+        project(pos01[:, 1, :], ANCHOR, 1, False, False)
+        project(neg01[:, 1, :], ANCHOR, 1, False, False)
+        project(anchors[:], ANCHOR, LONE, True, True)
+        project(pos23[:, 1, :], ANCHOR, 3, True, False)
+        project(neg3[:], ANCHOR, 3, True, False)
+        quantise(POSITIVE, 0, H)
+        quantise(POSITIVE, H, V)
+        project(pos01[:, 0, :], POSITIVE, 0, False, False)
+        project(pos01[:, 1, :], POSITIVE, 1, False, True)
         quantise(NEGATIVE, 0, H)
-        quantise(NEGATIVE, 3 * P, V)
-        alone[NEGATIVE] = psum.tile([P, N], F32, name="alone_negative", tag=f"bank{ANCHOR}")
-        project(alone[NEGATIVE][:], NEGATIVE, LONE, True, True)
-        project(neg0[:], NEGATIVE, 0, False, True)
-        project(neg1[:], NEGATIVE, 1, False, True)
-        project(neg3[:], NEGATIVE, 3, True, False)
-        project(neg3[:], ANCHOR, 3, False, True)
+        project(neg01[:, 0, :], NEGATIVE, 0, False, False)
+        project(neg01[:, 1, :], NEGATIVE, 1, False, True)
+        project(pos23[:, 0, :], POSITIVE, LONE, False, False)
+        project(pos23[:, 1, :], POSITIVE, 3, False, True)
+        quantise(NEGATIVE, H, V)
+        nc.scalar.copy(out=anchors_sb[:], in_=anchors[:])
+        negatives = psum.tile([P, N], F32, name="negatives", tag="bank5")
+        project(negatives[:], NEGATIVE, LONE, True, True)
+        project(neg3[:], NEGATIVE, 3, False, True)
 
-        nc.scalar.activation(out=near[:, 3, :], in_=pos3[:], func=ACT.Square)
         nc.scalar.activation(out=near[:, 0:2, :], in_=pos01[:], func=ACT.Square)
-        for c in (3,):
-            nc.scalar.activation(
-                out=minus_near[:, c, :], in_=near[:, c, :], func=ACT.Identity, scale=-1.0, bias=minus_margin[:, c : c + 1]
-            )
-        for c, acc in ((0, neg0), (1, neg1), (3, neg3)):
-            nc.scalar.activation(out=far[:, c, :], in_=acc[:], func=ACT.Square)
+        nc.scalar.activation(out=far[:, 0:2, :], in_=neg01[:], func=ACT.Square)
+        nc.scalar.activation(out=near[:, 3, :], in_=pos23[:, 1, :], func=ACT.Square)
+        nc.scalar.activation(out=far[:, 3, :], in_=neg3[:], func=ACT.Square)
 
-        for c in (0, 1):
+        def negate(c):
             nc.vector.tensor_scalar(
                 out=minus_near[:, c, :], in0=near[:, c, :], scalar1=-1.0, scalar2=minus_margin[:, c : c + 1], op0=ALU.mult, op1=ALU.add
             )
-        nc.vector.tensor_tensor(out=apart[:], in0=alone[NEGATIVE][:], in1=positives, op=ALU.subtract)
-        nc.vector.tensor_tensor(out=summed[:], in0=alone[NEGATIVE][:], in1=partial[:], op=ALU.add)
-        nc.vector.tensor_tensor(out=product[:], in0=apart[:], in1=summed[:], op=ALU.mult)
 
-        early = [psum.tile([P, H], F32, name=f"early{ft}", tag=tag) for ft, tag in enumerate(("bank2", "bank3"))]
-        for src in (minus_near, far):
-            for c in (0, 1):
-                for ft in range(2):
-                    first = src is minus_near and c == 0
-                    last = src is far and c == 1
-                    turn(early[ft][:, P * c : P * (c + 1)], src[:, c, P * ft : P * (ft + 1)], first, last)
-        for ft in range(2):
-            turn(late[ft][:, P : 2 * P], minus_near[:, 3, P * ft : P * (ft + 1)], False, False)
-        for ft in range(2):
-            turn(late[ft][:, P : 2 * P], far[:, 3, P * ft : P * (ft + 1)], False, False)
-        for ft in range(2):
-            turn(late[ft][:, 0:P], product[:, P * ft : P * (ft + 1)], False, True)
+        negate(0)
+        negate(1)
+        nc.vector.tensor_tensor(out=lone_pos[:], in0=pos23[:, 0, :], in1=anchors_sb[:], op=ALU.add)
+        nc.vector.tensor_tensor(out=lone_neg[:], in0=negatives[:], in1=anchors_sb[:], op=ALU.add)
+        nc.vector.scalar_tensor_tensor(
+            out=minus_near[:, LONE, :], in0=lone_pos[:], scalar=-1.0, in1=lone_pos[:], op0=ALU.mult, op1=ALU.mult
+        )
+        nc.vector.tensor_tensor(out=far[:, LONE, :], in0=lone_neg[:], in1=lone_neg[:], op=ALU.mult)
+        negate(3)
+
+        early = [psum.tile([P, H], F32, name=f"early{ft}", tag=f"bank{3 * ft}") for ft in range(2)]
+        for acc, chunks in ((early, (0, 1)), (late, (LONE, 3))):
+            for src in (minus_near, far):
+                for place, c in enumerate(chunks):
+                    for ft in range(2):
+                        first = acc is early and src is minus_near and place == 0
+                        last = src is far and place == 1
+                        turn(acc[ft][:, P * place : P * (place + 1)], src[:, c, P * ft : P * (ft + 1)], first, last)
         for acc, res, cols in ((early, result_early, slice(0, H)), (late, result_late, slice(H, V))):
             nc.vector.tensor_scalar(out=res[0][:], in0=acc[0][:], scalar1=-1.0, scalar2=0.0, op0=ALU.mult, op1=ALU.max)
             nc.sync.dma_start(out=out[0:P, cols], in_=res[0][:])

@@ -9,7 +9,7 @@ PACK = 4
 LIST_ROWS = 16
 ANCHOR, POSITIVE, NEGATIVE = 0, 1, 2
 H = V // 2
-LONE = 2
+LONE = 1
 FLOPS = 2 * K * N * S
 
 F32 = mybir.dt.float32
@@ -59,22 +59,26 @@ def tile_picked_triplet_none_e_kernel(tc, xT, w1_words, w1_scales, margin, offs,
         def entries(s0, s1):
             return offsets[:, s0 // LIST_ROWS : s1 // LIST_ROWS]
 
+        def gather(j, c0, c1):
+            nc.scalar.activation(
+                out=dense[j][:, c0:c1], in_=planes[j][:].indirect(entries(V + c0, V + c1)), func=ACT.Copy, scale=-1.0
+            )
+
+        def weave(copy, i, j, v0, v1):
+            first = (i - POSITIVE) * V
+            copy(out=picked[i][:, v0:v1, j], in_=dense[j][:, first + v0 : first + v1])
+
+        LAST = PACK - 1
         for j in range(PACK):
             nc.vector.tensor_copy(out=picked[ANCHOR][:, :, j], in_=planes[j][:].indirect(entries(0, V)))
-            last = j == PACK - 1
-            cuts = (0, V, V + H, 2 * V) if last else (0, 2 * V)
-            for c0, c1 in zip(cuts[:-1], cuts[1:]):
-                nc.scalar.activation(
-                    out=dense[j][:, c0:c1], in_=planes[j][:].indirect(entries(V + c0, V + c1)), func=ACT.Copy, scale=-1.0
-                )
-            halves = ((0, H), (H, V)) if last else ((0, V),)
-            for v0, v1 in halves:
-                nc.vector.tensor_copy(out=picked[POSITIVE][:, v0:v1, j], in_=dense[j][:, v0:v1])
-            for v0, v1 in halves:
-                if j < 2:
-                    nc.vector.tensor_copy(out=picked[NEGATIVE][:, v0:v1, j], in_=dense[j][:, V + v0 : V + v1])
-                else:
-                    nc.scalar.copy(out=picked[NEGATIVE][:, v0:v1, j], in_=dense[j][:, V + v0 : V + v1])
+            if j < LAST:
+                gather(j, 0, 2 * V)
+                weave(nc.vector.tensor_copy, POSITIVE, j, 0, V)
+                weave(nc.vector.tensor_copy if j < 2 else nc.scalar.copy, NEGATIVE, j, 0, V)
+        for c0 in range(0, 2 * V, H):
+            gather(LAST, c0, c0 + H)
+        for v0 in (0, H):
+            weave(nc.scalar.copy, NEGATIVE, LAST, v0, v0 + H)
 
         def quantise(i, v0, v1):
             nc.vector.quantize_mx(
@@ -102,77 +106,84 @@ def tile_picked_triplet_none_e_kernel(tc, xT, w1_words, w1_scales, margin, offs,
         for c in range(4):
             nc.tensor.transpose(turned_row[:, c, :], margin_row[:, P * c : P * (c + 1)], identity[:])
         nc.scalar.activation(out=minus_margin[:], in_=turned_row[:, :, 0], func=ACT.Copy, scale=-1.0)
-        late = [psum.tile([P, H], F32, name=f"late{ft}") for ft in range(2)]
+        early = [psum.tile([P, H], F32, name=f"early{ft}") for ft in range(2)]
         for ft in range(2):
-            turn(late[ft][:, 0:P], minus_margin[:, LONE : LONE + 1].to_broadcast([P, P]), True, False)
+            turn(early[ft][:, P : 2 * P], minus_margin[:, LONE : LONE + 1].to_broadcast([P, P]), True, False)
 
-        pos01 = psum.tile([P, 2, N], F32, name="pos01", tag="bank0")
-        pos23 = psum.tile([P, 2, N], F32, name="pos23", tag="bank1")
-        neg01 = psum.tile([P, 2, N], F32, name="neg01", tag="bank2")
-        neg3 = psum.tile([P, N], F32, name="neg3", tag="bank4")
-        anchors = psum.tile([P, N], F32, name="anchors", tag="bank5")
-        anchors_sb = keep.tile([P, N], F32, name="anchors_sb")
-        lone_pos = keep.tile([P, N], F32, name="lone_pos")
-        lone_neg = keep.tile([P, N], F32, name="lone_neg")
+        anchors = psum.tile([P, N], F32, name="anchors", tag="bank0")
+        pos01 = psum.tile([P, 2, N], F32, name="pos01", tag="bank1")
+        neg0 = psum.tile([P, N], F32, name="neg0", tag="bank2")
+        negatives = psum.tile([P, N], F32, name="negatives", tag="bank5")
+        pos23 = psum.tile([P, 2, N], F32, name="pos23", tag="bank3")
+        neg2 = psum.tile([P, N], F32, name="neg2", tag="bank4")
+        positives = keep.tile([P, N], F32, name="positives")
+        partial = keep.tile([P, N], F32, name="partial")
+        apart = keep.tile([P, N], F32, name="apart")
+        summed = keep.tile([P, N], F32, name="summed")
         near = keep.tile([P, 4, N], F32, name="near")
-        minus_near = keep.tile([P, 4, N], F32, name="minus_near")
         far = keep.tile([P, 4, N], F32, name="far")
+        minus_near = keep.tile([P, 4, N], F32, name="minus_near")
+        minus_loss = keep.tile([P, 3, N], F32, name="minus_loss")
         result_early = [keep.tile([P, H], F32, name=f"result_early{ft}") for ft in range(2)]
         result_late = [keep.tile([P, H], F32, name=f"result_late{ft}") for ft in range(2)]
 
         quantise(ANCHOR, 0, P)
         quantise(ANCHOR, P, H)
-        quantise(ANCHOR, H, V)
         project(pos01[:, 0, :], ANCHOR, 0, True, False)
-        project(neg01[:, 0, :], ANCHOR, 0, True, False)
-        project(pos01[:, 1, :], ANCHOR, 1, False, False)
-        project(neg01[:, 1, :], ANCHOR, 1, False, False)
+        project(neg0[:], ANCHOR, 0, True, False)
         project(anchors[:], ANCHOR, LONE, True, True)
-        project(pos23[:, 1, :], ANCHOR, 3, True, False)
-        project(neg3[:], ANCHOR, 3, True, False)
+        weave(nc.vector.tensor_copy, POSITIVE, LAST, 0, H)
+        quantise(ANCHOR, H, V)
+        project(pos23[:, 0, :], ANCHOR, 2, True, False)
+        project(pos23[:, 1, :], ANCHOR, 3, False, False)
         quantise(POSITIVE, 0, H)
-        quantise(POSITIVE, H, V)
         project(pos01[:, 0, :], POSITIVE, 0, False, False)
-        project(pos01[:, 1, :], POSITIVE, 1, False, True)
+        project(pos01[:, 1, :], POSITIVE, LONE, False, True)
+        weave(nc.vector.tensor_copy, POSITIVE, LAST, H, V)
         quantise(NEGATIVE, 0, H)
-        project(neg01[:, 0, :], NEGATIVE, 0, False, False)
-        project(neg01[:, 1, :], NEGATIVE, 1, False, True)
-        project(pos23[:, 0, :], POSITIVE, LONE, False, False)
+        project(negatives[:], NEGATIVE, LONE, True, True)
+        project(neg0[:], NEGATIVE, 0, False, True)
+        project(neg2[:], ANCHOR, 2, True, False)
+        quantise(POSITIVE, H, V)
+        project(pos23[:, 0, :], POSITIVE, 2, False, False)
         project(pos23[:, 1, :], POSITIVE, 3, False, True)
         quantise(NEGATIVE, H, V)
-        nc.scalar.copy(out=anchors_sb[:], in_=anchors[:])
-        negatives = psum.tile([P, N], F32, name="negatives", tag="bank5")
-        project(negatives[:], NEGATIVE, LONE, True, True)
-        project(neg3[:], NEGATIVE, 3, False, True)
+        project(neg2[:], NEGATIVE, 2, False, True)
+        nc.scalar.copy(out=positives[:], in_=pos01[:, LONE, :])
+        nc.vector.scalar_tensor_tensor(
+            out=partial[:], in0=anchors[:], scalar=2.0, in1=positives[:], op0=ALU.mult, op1=ALU.add
+        )
+        neg3 = psum.tile([P, N], F32, name="neg3", tag="bank0")
+        project(neg3[:], NEGATIVE, 3, True, False)
+        project(neg3[:], ANCHOR, 3, False, True)
 
-        nc.scalar.activation(out=near[:, 0:2, :], in_=pos01[:], func=ACT.Square)
-        nc.scalar.activation(out=far[:, 0:2, :], in_=neg01[:], func=ACT.Square)
-        nc.scalar.activation(out=near[:, 3, :], in_=pos23[:, 1, :], func=ACT.Square)
+        nc.scalar.activation(out=near[:, 0, :], in_=pos01[:, 0, :], func=ACT.Square)
+        nc.scalar.activation(out=far[:, 0, :], in_=neg0[:], func=ACT.Square)
+        nc.scalar.activation(out=near[:, 2:4, :], in_=pos23[:], func=ACT.Square)
+        nc.scalar.activation(out=far[:, 2, :], in_=neg2[:], func=ACT.Square)
         nc.scalar.activation(out=far[:, 3, :], in_=neg3[:], func=ACT.Square)
 
-        def negate(c):
+        nc.vector.tensor_tensor(out=apart[:], in0=negatives[:], in1=positives[:], op=ALU.subtract)
+        nc.vector.tensor_tensor(out=summed[:], in0=negatives[:], in1=partial[:], op=ALU.add)
+        nc.vector.scalar_tensor_tensor(
+            out=minus_loss[:, 0, :], in0=far[:, 0, :], scalar=minus_margin[:, 0:1], in1=near[:, 0, :], op0=ALU.add, op1=ALU.subtract
+        )
+        nc.vector.tensor_tensor(out=minus_loss[:, LONE, :], in0=apart[:], in1=summed[:], op=ALU.mult)
+        for c in (3,):
             nc.vector.tensor_scalar(
                 out=minus_near[:, c, :], in0=near[:, c, :], scalar1=-1.0, scalar2=minus_margin[:, c : c + 1], op0=ALU.mult, op1=ALU.add
             )
-
-        negate(0)
-        negate(1)
-        nc.vector.tensor_tensor(out=lone_pos[:], in0=pos23[:, 0, :], in1=anchors_sb[:], op=ALU.add)
-        nc.vector.tensor_tensor(out=lone_neg[:], in0=negatives[:], in1=anchors_sb[:], op=ALU.add)
         nc.vector.scalar_tensor_tensor(
-            out=minus_near[:, LONE, :], in0=lone_pos[:], scalar=-1.0, in1=lone_pos[:], op0=ALU.mult, op1=ALU.mult
+            out=minus_loss[:, 2, :], in0=far[:, 2, :], scalar=minus_margin[:, 2:3], in1=near[:, 2, :], op0=ALU.add, op1=ALU.subtract
         )
-        nc.vector.tensor_tensor(out=far[:, LONE, :], in0=lone_neg[:], in1=lone_neg[:], op=ALU.mult)
-        negate(3)
 
-        early = [psum.tile([P, H], F32, name=f"early{ft}", tag=f"bank{3 * ft}") for ft in range(2)]
-        for acc, chunks in ((early, (0, 1)), (late, (LONE, 3))):
-            for src in (minus_near, far):
-                for place, c in enumerate(chunks):
-                    for ft in range(2):
-                        first = acc is early and src is minus_near and place == 0
-                        last = src is far and place == 1
-                        turn(acc[ft][:, P * place : P * (place + 1)], src[:, c, P * ft : P * (ft + 1)], first, last)
+        for c in (0, LONE):
+            for ft in range(2):
+                turn(early[ft][:, P * c : P * (c + 1)], minus_loss[:, c, P * ft : P * (ft + 1)], False, c == LONE)
+        late = [psum.tile([P, H], F32, name=f"late{ft}", tag=f"bank{ft + 1}") for ft in range(2)]
+        for src, c in ((minus_near, 3), (minus_loss, 2), (far, 3)):
+            for ft in range(2):
+                turn(late[ft][:, P * (c - 2) : P * (c - 1)], src[:, c, P * ft : P * (ft + 1)], src is minus_near, src is far)
         for acc, res, cols in ((early, result_early, slice(0, H)), (late, result_late, slice(H, V))):
             nc.vector.tensor_scalar(out=res[0][:], in0=acc[0][:], scalar1=-1.0, scalar2=0.0, op0=ALU.mult, op1=ALU.max)
             nc.sync.dma_start(out=out[0:P, cols], in_=res[0][:])

@@ -35,9 +35,9 @@ def tile_picked_triplet_none_e_kernel(tc, xT, w1_words, w1_scales, margin, offs,
         identity = keep.tile([P, P], F32, name="identity")
         make_identity(nc, identity[:])
         planes = [keep.tile([P, T], F32, name=f"plane{j}") for j in range(PACK)]
-        dense = [keep.tile([P, 2 * V], BF16, name=f"dense{j}") for j in range(PACK)]
-        picked = [keep.tile([P, V, PACK], BF16, name=f"picked{i}", align_bytes=64) for i in range(3)]
-        words = [keep.tile([P, V], U32, name=f"words{i}", align_bytes=64) for i in range(3)]
+        dense = [keep.tile([P, S], BF16, name=f"dense{j}") for j in range(PACK)]
+        picked = [keep.tile([P, V, PACK], BF16, name=f"picked{i}", tag=f"picked{i}", align_bytes=64) for i in range(3)]
+        words = {(i, h): keep.tile([P, H], U32, name=f"words{i}{h}", align_bytes=64) for i in range(3) for h in range(2) if (i, h) != (NEGATIVE, 1)}
         scales = [keep.tile([P, V], U8, name=f"scales{i}", align_bytes=64) for i in range(3)]
 
         nc.vector.memset(w_scales[:].bitcast(I32), 0)
@@ -59,30 +59,40 @@ def tile_picked_triplet_none_e_kernel(tc, xT, w1_words, w1_scales, margin, offs,
         def entries(s0, s1):
             return offsets[:, s0 // LIST_ROWS : s1 // LIST_ROWS]
 
-        def gather(j, c0, c1):
+        def gather(i, j, v0, v1):
+            s0, s1 = i * V + v0, i * V + v1
             nc.scalar.activation(
-                out=dense[j][:, c0:c1], in_=planes[j][:].indirect(entries(V + c0, V + c1)), func=ACT.Copy, scale=-1.0
+                out=dense[j][:, s0:s1],
+                in_=planes[j][:].indirect(entries(s0, s1)),
+                func=ACT.Copy,
+                scale=1.0 if i == ANCHOR else -1.0,
             )
 
         def weave(copy, i, j, v0, v1):
-            first = (i - POSITIVE) * V
-            copy(out=picked[i][:, v0:v1, j], in_=dense[j][:, first + v0 : first + v1])
+            copy(out=picked[i][:, v0:v1, j], in_=dense[j][:, i * V + v0 : i * V + v1])
 
         LAST = PACK - 1
-        for j in range(PACK):
+        for j in range(LAST):
             nc.vector.tensor_copy(out=picked[ANCHOR][:, :, j], in_=planes[j][:].indirect(entries(0, V)))
-            if j < LAST:
-                gather(j, 0, 2 * V)
-                weave(nc.vector.tensor_copy, POSITIVE, j, 0, V)
-                weave(nc.vector.tensor_copy if j < 2 else nc.scalar.copy, NEGATIVE, j, 0, V)
-        for c0 in range(0, 2 * V, H):
-            gather(LAST, c0, c0 + H)
-        for v0 in (0, H):
-            weave(nc.scalar.copy, NEGATIVE, LAST, v0, v0 + H)
+            gather(POSITIVE, j, 0, 2 * V)
+            weave(nc.vector.tensor_copy, POSITIVE, j, 0, V)
+            if j < 2:
+                weave(nc.vector.tensor_copy, NEGATIVE, j, 0, V)
+            else:
+                weave(nc.vector.tensor_copy, NEGATIVE, j, 0, H)
+                weave(nc.scalar.copy, NEGATIVE, j, H, V)
+        for v0 in (0, P):
+            nc.vector.tensor_copy(out=dense[LAST][:, v0 : v0 + P], in_=planes[LAST][:].indirect(entries(v0, v0 + P)))
+        for i, v0 in ((POSITIVE, 0), (NEGATIVE, 0), (ANCHOR, H), (POSITIVE, H)):
+            gather(i, LAST, v0, v0 + H)
+        for v0 in (H, H + P):
+            gather(NEGATIVE, LAST, v0, v0 + P)
+        for v0 in (H, H + P):
+            weave(nc.scalar.copy, NEGATIVE, LAST, v0, v0 + P)
 
         def quantise(i, v0, v1):
             nc.vector.quantize_mx(
-                out=words[i][:, v0:v1].bitcast(FP8X4),
+                out=words[i, v0 // H][:, v0 % H : v0 % H + v1 - v0].bitcast(FP8X4),
                 scales=scales[i][:, v0:v1],
                 in_=picked[i][:, v0:v1, :].rearrange("p v j -> p (v j)"),
             )
@@ -90,7 +100,7 @@ def tile_picked_triplet_none_e_kernel(tc, xT, w1_words, w1_scales, margin, offs,
         def project(acc, i, c, start, stop):
             nc.tensor.matmul_mx(
                 out=acc,
-                lhsT=words[i][:, P * c : P * (c + 1)].bitcast(FP8X4),
+                lhsT=words[i, c // 2][:, P * (c % 2) : P * (c % 2 + 1)].bitcast(FP8X4),
                 lhsT_scale=scales[i][:, P * c : P * (c + 1)],
                 rhs=w_words[:].bitcast(FP8X4),
                 rhs_scale=w_scales[:],
@@ -117,41 +127,46 @@ def tile_picked_triplet_none_e_kernel(tc, xT, w1_words, w1_scales, margin, offs,
         pos23 = psum.tile([P, 2, N], F32, name="pos23", tag="bank3")
         neg2 = psum.tile([P, N], F32, name="neg2", tag="bank4")
         positives = keep.tile([P, N], F32, name="positives")
-        partial = keep.tile([P, N], F32, name="partial")
-        apart = keep.tile([P, N], F32, name="apart")
         summed = keep.tile([P, N], F32, name="summed")
         near = keep.tile([P, 4, N], F32, name="near")
         far = keep.tile([P, 4, N], F32, name="far")
         minus_near = keep.tile([P, 4, N], F32, name="minus_near")
-        minus_loss = keep.tile([P, 3, N], F32, name="minus_loss")
         result_early = [keep.tile([P, H], F32, name=f"result_early{ft}") for ft in range(2)]
         result_late = [keep.tile([P, H], F32, name=f"result_late{ft}") for ft in range(2)]
 
+        for v0 in (0, P):
+            weave(nc.vector.tensor_copy, ANCHOR, LAST, v0, v0 + P)
         quantise(ANCHOR, 0, P)
         quantise(ANCHOR, P, H)
         project(pos01[:, 0, :], ANCHOR, 0, True, False)
         project(neg0[:], ANCHOR, 0, True, False)
         project(anchors[:], ANCHOR, LONE, True, True)
         weave(nc.vector.tensor_copy, POSITIVE, LAST, 0, H)
-        quantise(ANCHOR, H, V)
-        project(pos23[:, 0, :], ANCHOR, 2, True, False)
-        project(pos23[:, 1, :], ANCHOR, 3, False, False)
+        weave(nc.vector.tensor_copy, NEGATIVE, LAST, 0, H)
         quantise(POSITIVE, 0, H)
         project(pos01[:, 0, :], POSITIVE, 0, False, False)
         project(pos01[:, 1, :], POSITIVE, LONE, False, True)
-        weave(nc.vector.tensor_copy, POSITIVE, LAST, H, V)
         quantise(NEGATIVE, 0, H)
         project(negatives[:], NEGATIVE, LONE, True, True)
         project(neg0[:], NEGATIVE, 0, False, True)
+        weave(nc.vector.tensor_copy, ANCHOR, LAST, H, V)
+        weave(nc.vector.tensor_copy, POSITIVE, LAST, H, V)
+        quantise(ANCHOR, H, V)
+        project(pos23[:, 0, :], ANCHOR, 2, True, False)
+        project(pos23[:, 1, :], ANCHOR, 3, False, False)
         project(neg2[:], ANCHOR, 2, True, False)
         quantise(POSITIVE, H, V)
         project(pos23[:, 0, :], POSITIVE, 2, False, False)
         project(pos23[:, 1, :], POSITIVE, 3, False, True)
+        words[NEGATIVE, 1] = keep.tile([P, H], U32, name="words_last", tag=f"picked{ANCHOR}", align_bytes=64)
         quantise(NEGATIVE, H, V)
+        factors = keep.tile([P, 2, N], F32, name="factors", tag=f"picked{POSITIVE}", align_bytes=64)
+        partial, apart = factors[:, 0, :], factors[:, 1, :]
+        minus_loss = keep.tile([P, 3, N], F32, name="minus_loss", tag=f"picked{NEGATIVE}", align_bytes=64)
         project(neg2[:], NEGATIVE, 2, False, True)
         nc.scalar.copy(out=positives[:], in_=pos01[:, LONE, :])
         nc.vector.scalar_tensor_tensor(
-            out=partial[:], in0=anchors[:], scalar=2.0, in1=positives[:], op0=ALU.mult, op1=ALU.add
+            out=partial, in0=anchors[:], scalar=2.0, in1=positives[:], op0=ALU.mult, op1=ALU.add
         )
         neg3 = psum.tile([P, N], F32, name="neg3", tag="bank0")
         project(neg3[:], NEGATIVE, 3, True, False)
@@ -163,12 +178,12 @@ def tile_picked_triplet_none_e_kernel(tc, xT, w1_words, w1_scales, margin, offs,
         nc.scalar.activation(out=far[:, 2, :], in_=neg2[:], func=ACT.Square)
         nc.scalar.activation(out=far[:, 3, :], in_=neg3[:], func=ACT.Square)
 
-        nc.vector.tensor_tensor(out=apart[:], in0=negatives[:], in1=positives[:], op=ALU.subtract)
-        nc.vector.tensor_tensor(out=summed[:], in0=negatives[:], in1=partial[:], op=ALU.add)
+        nc.vector.tensor_tensor(out=apart, in0=negatives[:], in1=positives[:], op=ALU.subtract)
+        nc.vector.tensor_tensor(out=summed[:], in0=negatives[:], in1=partial, op=ALU.add)
         nc.vector.scalar_tensor_tensor(
             out=minus_loss[:, 0, :], in0=far[:, 0, :], scalar=minus_margin[:, 0:1], in1=near[:, 0, :], op0=ALU.add, op1=ALU.subtract
         )
-        nc.vector.tensor_tensor(out=minus_loss[:, LONE, :], in0=apart[:], in1=summed[:], op=ALU.mult)
+        nc.vector.tensor_tensor(out=minus_loss[:, LONE, :], in0=apart, in1=summed[:], op=ALU.mult)
         for c in (3,):
             nc.vector.tensor_scalar(
                 out=minus_near[:, c, :], in0=near[:, c, :], scalar1=-1.0, scalar2=minus_margin[:, c : c + 1], op0=ALU.mult, op1=ALU.add

@@ -9,7 +9,7 @@ PACK = 4
 LIST_ROWS = 16
 ANCHOR, POSITIVE, NEGATIVE = 0, 1, 2
 H = V // 2
-LONE = 1
+LONE = 2
 FLOPS = 2 * K * N * S
 
 F32 = mybir.dt.float32
@@ -37,7 +37,7 @@ def tile_picked_triplet_none_e_kernel(tc, xT, w1_words, w1_scales, margin, offs,
         planes = [keep.tile([P, T], F32, name=f"plane{j}") for j in range(PACK)]
         dense = [keep.tile([P, S], BF16, name=f"dense{j}") for j in range(PACK)]
         picked = [keep.tile([P, V, PACK], BF16, name=f"picked{i}", tag=f"picked{i}", align_bytes=64) for i in range(3)]
-        words = {(i, h): keep.tile([P, H], U32, name=f"words{i}{h}", align_bytes=64) for i in range(3) for h in range(2) if (i, h) != (NEGATIVE, 1)}
+        words = {(i, h): keep.tile([P, H], U32, name=f"words{i}{h}", tag=f"words{i}{h}", align_bytes=64) for i in range(3) for h in range(2) if (i, h) != (NEGATIVE, 1)}
         scales = [keep.tile([P, V], U8, name=f"scales{i}", align_bytes=64) for i in range(3)]
 
         nc.vector.memset(w_scales[:].bitcast(I32), 0)
@@ -83,7 +83,7 @@ def tile_picked_triplet_none_e_kernel(tc, xT, w1_words, w1_scales, margin, offs,
                 weave(nc.scalar.copy, NEGATIVE, j, H, V)
         for v0 in (0, P):
             nc.vector.tensor_copy(out=dense[LAST][:, v0 : v0 + P], in_=planes[LAST][:].indirect(entries(v0, v0 + P)))
-        for i, v0 in ((POSITIVE, 0), (NEGATIVE, 0), (ANCHOR, H), (POSITIVE, H)):
+        for i, v0 in ((POSITIVE, 0), (NEGATIVE, 0), (POSITIVE, H), (ANCHOR, H)):
             gather(i, LAST, v0, v0 + H)
         for v0 in (H, H + P):
             gather(NEGATIVE, LAST, v0, v0 + P)
@@ -116,21 +116,21 @@ def tile_picked_triplet_none_e_kernel(tc, xT, w1_words, w1_scales, margin, offs,
         for c in range(4):
             nc.tensor.transpose(turned_row[:, c, :], margin_row[:, P * c : P * (c + 1)], identity[:])
         nc.scalar.activation(out=minus_margin[:], in_=turned_row[:, :, 0], func=ACT.Copy, scale=-1.0)
-        early = [psum.tile([P, H], F32, name=f"early{ft}") for ft in range(2)]
+        late = [psum.tile([P, H], F32, name=f"late{ft}") for ft in range(2)]
         for ft in range(2):
-            turn(early[ft][:, P : 2 * P], minus_margin[:, LONE : LONE + 1].to_broadcast([P, P]), True, False)
+            turn(late[ft][:, 0:P], minus_margin[:, LONE : LONE + 1].to_broadcast([P, P]), True, False)
 
-        anchors = psum.tile([P, N], F32, name="anchors", tag="bank0")
-        pos01 = psum.tile([P, 2, N], F32, name="pos01", tag="bank1")
-        neg0 = psum.tile([P, N], F32, name="neg0", tag="bank2")
-        negatives = psum.tile([P, N], F32, name="negatives", tag="bank5")
-        pos23 = psum.tile([P, 2, N], F32, name="pos23", tag="bank3")
-        neg2 = psum.tile([P, N], F32, name="neg2", tag="bank4")
+        pos01 = psum.tile([P, 2, N], F32, name="pos01", tag="bank0")
+        neg01 = psum.tile([P, 2, N], F32, name="neg01", tag="bank1")
+        anchors = psum.tile([P, N], F32, name="anchors", tag="bank2")
+        lone_pos = psum.tile([P, N], F32, name="lone_pos", tag="bank3")
+        pos3 = psum.tile([P, N], F32, name="pos3", tag="bank5")
+        neg3 = psum.tile([P, N], F32, name="neg3", tag="bank4")
         positives = keep.tile([P, N], F32, name="positives")
         summed = keep.tile([P, N], F32, name="summed")
+        product = keep.tile([P, N], F32, name="product")
         near = keep.tile([P, 4, N], F32, name="near")
-        far = keep.tile([P, 4, N], F32, name="far")
-        minus_near = keep.tile([P, 4, N], F32, name="minus_near")
+        far3 = keep.tile([P, N], F32, name="far3")
         result_early = [keep.tile([P, H], F32, name=f"result_early{ft}") for ft in range(2)]
         result_late = [keep.tile([P, H], F32, name=f"result_late{ft}") for ft in range(2)]
 
@@ -139,68 +139,72 @@ def tile_picked_triplet_none_e_kernel(tc, xT, w1_words, w1_scales, margin, offs,
         quantise(ANCHOR, 0, P)
         quantise(ANCHOR, P, H)
         project(pos01[:, 0, :], ANCHOR, 0, True, False)
-        project(neg0[:], ANCHOR, 0, True, False)
-        project(anchors[:], ANCHOR, LONE, True, True)
+        project(neg01[:, 0, :], ANCHOR, 0, True, False)
+        project(pos01[:, 1, :], ANCHOR, 1, False, False)
+        project(neg01[:, 1, :], ANCHOR, 1, False, False)
         weave(nc.vector.tensor_copy, POSITIVE, LAST, 0, H)
         weave(nc.vector.tensor_copy, NEGATIVE, LAST, 0, H)
         quantise(POSITIVE, 0, H)
         project(pos01[:, 0, :], POSITIVE, 0, False, False)
-        project(pos01[:, 1, :], POSITIVE, LONE, False, True)
+        project(pos01[:, 1, :], POSITIVE, 1, False, True)
         quantise(NEGATIVE, 0, H)
-        project(negatives[:], NEGATIVE, LONE, True, True)
-        project(neg0[:], NEGATIVE, 0, False, True)
-        weave(nc.vector.tensor_copy, ANCHOR, LAST, H, V)
+        project(neg01[:, 0, :], NEGATIVE, 0, False, False)
+        project(neg01[:, 1, :], NEGATIVE, 1, False, True)
         weave(nc.vector.tensor_copy, POSITIVE, LAST, H, V)
-        quantise(ANCHOR, H, V)
-        project(pos23[:, 0, :], ANCHOR, 2, True, False)
-        project(pos23[:, 1, :], ANCHOR, 3, False, False)
-        project(neg2[:], ANCHOR, 2, True, False)
+        weave(nc.vector.tensor_copy, ANCHOR, LAST, H, V)
         quantise(POSITIVE, H, V)
-        project(pos23[:, 0, :], POSITIVE, 2, False, False)
-        project(pos23[:, 1, :], POSITIVE, 3, False, True)
-        words[NEGATIVE, 1] = keep.tile([P, H], U32, name="words_last", tag=f"picked{ANCHOR}", align_bytes=64)
+        project(lone_pos[:], POSITIVE, LONE, True, True)
+        project(pos3[:], POSITIVE, 3, True, False)
+        quantise(ANCHOR, H, V)
+        project(anchors[:], ANCHOR, LONE, True, True)
+        project(pos3[:], ANCHOR, 3, False, True)
+        project(neg3[:], ANCHOR, 3, True, False)
+        words[NEGATIVE, 1] = keep.tile([P, H], U32, name="words_last", tag=f"picked{POSITIVE}", align_bytes=64)
         quantise(NEGATIVE, H, V)
-        factors = keep.tile([P, 2, N], F32, name="factors", tag=f"picked{POSITIVE}", align_bytes=64)
+        project(neg3[:], NEGATIVE, 3, False, True)
+
+        nc.scalar.activation(out=near[:, 0:2, :], in_=pos01[:], func=ACT.Square)
+        nc.scalar.copy(out=positives[:], in_=lone_pos[:])
+        negatives = psum.tile([P, N], F32, name="negatives", tag="bank3")
+        project(negatives[:], NEGATIVE, LONE, True, True)
+        far01 = keep.tile([P, 2, N], F32, name="far01", tag=f"words{POSITIVE}1", align_bytes=64)
+        nc.scalar.activation(out=far01[:], in_=neg01[:], func=ACT.Square)
+        nc.scalar.activation(out=near[:, 3, :], in_=pos3[:], func=ACT.Square)
+        nc.scalar.activation(out=far3[:], in_=neg3[:], func=ACT.Square)
+
+        minus_near = keep.tile([P, 4, N], F32, name="minus_near", tag=f"picked{ANCHOR}", align_bytes=64)
+        factors = keep.tile([P, 2, N], F32, name="factors", tag=f"picked{NEGATIVE}", align_bytes=64)
         partial, apart = factors[:, 0, :], factors[:, 1, :]
-        minus_loss = keep.tile([P, 3, N], F32, name="minus_loss", tag=f"picked{NEGATIVE}", align_bytes=64)
-        project(neg2[:], NEGATIVE, 2, False, True)
-        nc.scalar.copy(out=positives[:], in_=pos01[:, LONE, :])
-        nc.vector.scalar_tensor_tensor(
-            out=partial, in0=anchors[:], scalar=2.0, in1=positives[:], op0=ALU.mult, op1=ALU.add
-        )
-        neg3 = psum.tile([P, N], F32, name="neg3", tag="bank0")
-        project(neg3[:], NEGATIVE, 3, True, False)
-        project(neg3[:], ANCHOR, 3, False, True)
 
-        nc.scalar.activation(out=near[:, 0, :], in_=pos01[:, 0, :], func=ACT.Square)
-        nc.scalar.activation(out=far[:, 0, :], in_=neg0[:], func=ACT.Square)
-        nc.scalar.activation(out=near[:, 2:4, :], in_=pos23[:], func=ACT.Square)
-        nc.scalar.activation(out=far[:, 2, :], in_=neg2[:], func=ACT.Square)
-        nc.scalar.activation(out=far[:, 3, :], in_=neg3[:], func=ACT.Square)
-
-        nc.vector.tensor_tensor(out=apart, in0=negatives[:], in1=positives[:], op=ALU.subtract)
-        nc.vector.tensor_tensor(out=summed[:], in0=negatives[:], in1=partial, op=ALU.add)
-        nc.vector.scalar_tensor_tensor(
-            out=minus_loss[:, 0, :], in0=far[:, 0, :], scalar=minus_margin[:, 0:1], in1=near[:, 0, :], op0=ALU.add, op1=ALU.subtract
-        )
-        nc.vector.tensor_tensor(out=minus_loss[:, LONE, :], in0=apart, in1=summed[:], op=ALU.mult)
-        for c in (3,):
+        def negate(c):
             nc.vector.tensor_scalar(
                 out=minus_near[:, c, :], in0=near[:, c, :], scalar1=-1.0, scalar2=minus_margin[:, c : c + 1], op0=ALU.mult, op1=ALU.add
             )
-        nc.vector.scalar_tensor_tensor(
-            out=minus_loss[:, 2, :], in0=far[:, 2, :], scalar=minus_margin[:, 2:3], in1=near[:, 2, :], op0=ALU.add, op1=ALU.subtract
-        )
 
-        for c in (0, LONE):
+        negate(0)
+        negate(1)
+        nc.vector.scalar_tensor_tensor(
+            out=partial, in0=anchors[:], scalar=2.0, in1=positives[:], op0=ALU.mult, op1=ALU.add
+        )
+        nc.vector.tensor_tensor(out=apart, in0=negatives[:], in1=positives[:], op=ALU.subtract)
+        nc.vector.tensor_tensor(out=summed[:], in0=negatives[:], in1=partial, op=ALU.add)
+        negate(3)
+        nc.vector.tensor_tensor(out=product[:], in0=apart, in1=summed[:], op=ALU.mult)
+
+        early = [psum.tile([P, H], F32, name=f"early{ft}", tag=f"bank{ft}") for ft in range(2)]
+        for ft in range(2):
+            for src in (minus_near, far01):
+                for c in (0, 1):
+                    first = src is minus_near and c == 0
+                    last = src is far01 and c == 1
+                    turn(early[ft][:, P * c : P * (c + 1)], src[:, c, P * ft : P * (ft + 1)], first, last)
+        for src, place in ((minus_near[:, 3, :], 1), (far3[:], 1), (product[:], 0)):
             for ft in range(2):
-                turn(early[ft][:, P * c : P * (c + 1)], minus_loss[:, c, P * ft : P * (ft + 1)], False, c == LONE)
-        late = [psum.tile([P, H], F32, name=f"late{ft}", tag=f"bank{ft + 1}") for ft in range(2)]
-        for src, c in ((minus_near, 3), (minus_loss, 2), (far, 3)):
-            for ft in range(2):
-                turn(late[ft][:, P * (c - 2) : P * (c - 1)], src[:, c, P * ft : P * (ft + 1)], src is minus_near, src is far)
-        for acc, res, cols in ((early, result_early, slice(0, H)), (late, result_late, slice(H, V))):
-            nc.vector.tensor_scalar(out=res[0][:], in0=acc[0][:], scalar1=-1.0, scalar2=0.0, op0=ALU.mult, op1=ALU.max)
-            nc.sync.dma_start(out=out[0:P, cols], in_=res[0][:])
-            nc.scalar.activation(out=res[1][:], in_=acc[1][:], func=ACT.Relu, scale=-1.0)
-            (nc.sync if acc is early else nc.scalar).dma_start(out=out[P : 2 * P, cols], in_=res[1][:])
+                turn(late[ft][:, P * place : P * (place + 1)], src[:, P * ft : P * (ft + 1)], False, place == 0)
+        for ft in range(2):
+            nc.scalar.activation(out=result_early[ft][:], in_=early[ft][:], func=ACT.Relu, scale=-1.0)
+            nc.sync.dma_start(out=out[P * ft : P * (ft + 1), 0:H], in_=result_early[ft][:])
+        nc.vector.tensor_scalar(out=result_late[0][:], in0=late[0][:], scalar1=-1.0, scalar2=0.0, op0=ALU.mult, op1=ALU.max)
+        nc.sync.dma_start(out=out[0:P, H:V], in_=result_late[0][:])
+        nc.scalar.activation(out=result_late[1][:], in_=late[1][:], func=ACT.Relu, scale=-1.0)
+        nc.scalar.dma_start(out=out[P : 2 * P, H:V], in_=result_late[1][:])

@@ -10,6 +10,7 @@ LIST_ROWS = 16
 ANCHOR, POSITIVE, NEGATIVE = 0, 1, 2
 H = V // 2
 LONE = 2
+SPLIT = 448
 FLOPS = 2 * K * N * S
 
 F32 = mybir.dt.float32
@@ -35,7 +36,7 @@ def tile_picked_triplet_none_e_kernel(tc, xT, w1_words, w1_scales, margin, offs,
         identity = keep.tile([P, P], F32, name="identity")
         make_identity(nc, identity[:])
         planes = [keep.tile([P, T], F32, name=f"plane{j}") for j in range(PACK)]
-        dense = [keep.tile([P, S], BF16, name=f"dense{j}") for j in range(PACK)]
+        dense = [keep.tile([P, S], BF16, name=f"dense{j}", tag=f"dense{j}") for j in range(PACK)]
         picked = [keep.tile([P, V, PACK], BF16, name=f"picked{i}", tag=f"picked{i}", align_bytes=64) for i in range(3)]
         words = {(i, h): keep.tile([P, H], U32, name=f"words{i}{h}", tag=f"words{i}{h}", align_bytes=64) for i in range(3) for h in range(2) if (i, h) != (NEGATIVE, 1)}
         scales = [keep.tile([P, V], U8, name=f"scales{i}", align_bytes=64) for i in range(3)]
@@ -80,15 +81,16 @@ def tile_picked_triplet_none_e_kernel(tc, xT, w1_words, w1_scales, margin, offs,
                 weave(nc.vector.tensor_copy, NEGATIVE, j, 0, V)
             else:
                 weave(nc.vector.tensor_copy, NEGATIVE, j, 0, H)
-                weave(nc.scalar.copy, NEGATIVE, j, H, V)
+                weave(nc.vector.tensor_copy, NEGATIVE, j, SPLIT, V)
+                weave(nc.scalar.copy, NEGATIVE, j, H, SPLIT)
         for v0 in (0, P):
             nc.vector.tensor_copy(out=dense[LAST][:, v0 : v0 + P], in_=planes[LAST][:].indirect(entries(v0, v0 + P)))
-        for i, v0 in ((POSITIVE, 0), (NEGATIVE, 0), (POSITIVE, H), (ANCHOR, H)):
+        for i, v0 in ((POSITIVE, 0), (NEGATIVE, 0), (ANCHOR, H), (POSITIVE, H)):
             gather(i, LAST, v0, v0 + H)
         for v0 in (H, H + P):
             gather(NEGATIVE, LAST, v0, v0 + P)
-        for v0 in (H, H + P):
-            weave(nc.scalar.copy, NEGATIVE, LAST, v0, v0 + P)
+        for v0, v1 in ((H, H + P), (H + P, SPLIT)):
+            weave(nc.scalar.copy, NEGATIVE, LAST, v0, v1)
 
         def quantise(i, v0, v1):
             nc.vector.quantize_mx(
@@ -116,21 +118,22 @@ def tile_picked_triplet_none_e_kernel(tc, xT, w1_words, w1_scales, margin, offs,
         for c in range(4):
             nc.tensor.transpose(turned_row[:, c, :], margin_row[:, P * c : P * (c + 1)], identity[:])
         nc.scalar.activation(out=minus_margin[:], in_=turned_row[:, :, 0], func=ACT.Copy, scale=-1.0)
+        def add_margin(acc, c, start):
+            turn(acc[:, P * (c % 2) : P * (c % 2 + 1)], minus_margin[:, c : c + 1].to_broadcast([P, P]), start, False)
+
         late = [psum.tile([P, H], F32, name=f"late{ft}") for ft in range(2)]
         for ft in range(2):
-            turn(late[ft][:, 0:P], minus_margin[:, LONE : LONE + 1].to_broadcast([P, P]), True, False)
+            add_margin(late[ft], 2, True)
+            add_margin(late[ft], 3, False)
 
         pos01 = psum.tile([P, 2, N], F32, name="pos01", tag="bank0")
         neg01 = psum.tile([P, 2, N], F32, name="neg01", tag="bank1")
-        anchors = psum.tile([P, N], F32, name="anchors", tag="bank2")
-        lone_pos = psum.tile([P, N], F32, name="lone_pos", tag="bank3")
-        pos3 = psum.tile([P, N], F32, name="pos3", tag="bank5")
-        neg3 = psum.tile([P, N], F32, name="neg3", tag="bank4")
-        positives = keep.tile([P, N], F32, name="positives")
-        summed = keep.tile([P, N], F32, name="summed")
-        product = keep.tile([P, N], F32, name="product")
+        lone = {i: psum.tile([P, N], F32, name=f"lone{i}", tag=tag) for i, tag in enumerate(("bank2", "bank3", "bank5"))}
+        last = psum.tile([P, 2, N], F32, name="last", tag="bank4")
+        pos3, neg3 = last[:, 0, :], last[:, 1, :]
+        anchors = keep.tile([P, N], F32, name="anchors")
         near = keep.tile([P, 4, N], F32, name="near")
-        far3 = keep.tile([P, N], F32, name="far3")
+        far23 = keep.tile([P, 2, N], F32, name="far23")
         result_early = [keep.tile([P, H], F32, name=f"result_early{ft}") for ft in range(2)]
         result_late = [keep.tile([P, H], F32, name=f"result_late{ft}") for ft in range(2)]
 
@@ -141,7 +144,6 @@ def tile_picked_triplet_none_e_kernel(tc, xT, w1_words, w1_scales, margin, offs,
         project(pos01[:, 0, :], ANCHOR, 0, True, False)
         project(neg01[:, 0, :], ANCHOR, 0, True, False)
         project(pos01[:, 1, :], ANCHOR, 1, False, False)
-        project(neg01[:, 1, :], ANCHOR, 1, False, False)
         weave(nc.vector.tensor_copy, POSITIVE, LAST, 0, H)
         weave(nc.vector.tensor_copy, NEGATIVE, LAST, 0, H)
         quantise(POSITIVE, 0, H)
@@ -149,62 +151,57 @@ def tile_picked_triplet_none_e_kernel(tc, xT, w1_words, w1_scales, margin, offs,
         project(pos01[:, 1, :], POSITIVE, 1, False, True)
         quantise(NEGATIVE, 0, H)
         project(neg01[:, 0, :], NEGATIVE, 0, False, False)
-        project(neg01[:, 1, :], NEGATIVE, 1, False, True)
-        weave(nc.vector.tensor_copy, POSITIVE, LAST, H, V)
+        project(neg01[:, 1, :], NEGATIVE, 1, False, False)
+        project(neg01[:, 1, :], ANCHOR, 1, False, True)
         weave(nc.vector.tensor_copy, ANCHOR, LAST, H, V)
-        quantise(POSITIVE, H, V)
-        project(lone_pos[:], POSITIVE, LONE, True, True)
-        project(pos3[:], POSITIVE, 3, True, False)
+        weave(nc.vector.tensor_copy, POSITIVE, LAST, H, V)
         quantise(ANCHOR, H, V)
-        project(anchors[:], ANCHOR, LONE, True, True)
-        project(pos3[:], ANCHOR, 3, False, True)
-        project(neg3[:], ANCHOR, 3, True, False)
-        words[NEGATIVE, 1] = keep.tile([P, H], U32, name="words_last", tag=f"picked{POSITIVE}", align_bytes=64)
+        project(lone[ANCHOR][:], ANCHOR, LONE, True, True)
+        project(pos3, ANCHOR, 3, True, False)
+        project(neg3, ANCHOR, 3, False, False)
+        weave(nc.vector.tensor_copy, NEGATIVE, LAST, SPLIT, V)
+        quantise(POSITIVE, H, V)
+        project(lone[POSITIVE][:], POSITIVE, LONE, True, True)
+        project(pos3, POSITIVE, 3, False, False)
+        words[NEGATIVE, 1] = keep.tile([P, H], U32, name="words_last", tag=f"picked{ANCHOR}", align_bytes=64)
         quantise(NEGATIVE, H, V)
-        project(neg3[:], NEGATIVE, 3, False, True)
+        project(lone[NEGATIVE][:], NEGATIVE, LONE, True, True)
+        project(neg3, NEGATIVE, 3, False, True)
 
         nc.scalar.activation(out=near[:, 0:2, :], in_=pos01[:], func=ACT.Square)
-        nc.scalar.copy(out=positives[:], in_=lone_pos[:])
-        negatives = psum.tile([P, N], F32, name="negatives", tag="bank3")
-        project(negatives[:], NEGATIVE, LONE, True, True)
-        far01 = keep.tile([P, 2, N], F32, name="far01", tag=f"words{POSITIVE}1", align_bytes=64)
-        nc.scalar.activation(out=far01[:], in_=neg01[:], func=ACT.Square)
-        nc.scalar.activation(out=near[:, 3, :], in_=pos3[:], func=ACT.Square)
-        nc.scalar.activation(out=far3[:], in_=neg3[:], func=ACT.Square)
+        far0 = keep.tile([P, N], F32, name="far0")
+        nc.scalar.activation(out=far0[:], in_=neg01[:, 0, :], func=ACT.Square)
+        nc.scalar.copy(out=anchors[:], in_=lone[ANCHOR][:])
+        far1 = keep.tile([P, N], F32, name="far1", tag=f"words{ANCHOR}1", align_bytes=64)
+        nc.scalar.activation(out=far1[:], in_=neg01[:, 1, :], func=ACT.Square)
+        nc.scalar.activation(out=near[:, 3, :], in_=pos3, func=ACT.Square)
+        nc.scalar.activation(out=far23[:, 1, :], in_=neg3, func=ACT.Square)
 
-        minus_near = keep.tile([P, 4, N], F32, name="minus_near", tag=f"picked{ANCHOR}", align_bytes=64)
-        factors = keep.tile([P, 2, N], F32, name="factors", tag=f"picked{NEGATIVE}", align_bytes=64)
-        partial, apart = factors[:, 0, :], factors[:, 1, :]
-
-        def negate(c):
+        minus_near = keep.tile([P, 4, N], F32, name="minus_near", tag=f"picked{POSITIVE}", align_bytes=64)
+        apart = keep.tile([P, 2, N], F32, name="apart", tag=f"picked{NEGATIVE}", align_bytes=64)
+        for c in (0, 1):
             nc.vector.tensor_scalar(
                 out=minus_near[:, c, :], in0=near[:, c, :], scalar1=-1.0, scalar2=minus_margin[:, c : c + 1], op0=ALU.mult, op1=ALU.add
             )
-
-        negate(0)
-        negate(1)
+        for place, i in enumerate((POSITIVE, NEGATIVE)):
+            nc.vector.tensor_tensor(out=apart[:, place, :], in0=lone[i][:], in1=anchors[:], op=ALU.add)
         nc.vector.scalar_tensor_tensor(
-            out=partial, in0=anchors[:], scalar=2.0, in1=positives[:], op0=ALU.mult, op1=ALU.add
+            out=minus_near[:, LONE, :], in0=apart[:, 0, :], scalar=-1.0, in1=apart[:, 0, :], op0=ALU.mult, op1=ALU.mult
         )
-        nc.vector.tensor_tensor(out=apart, in0=negatives[:], in1=positives[:], op=ALU.subtract)
-        nc.vector.tensor_tensor(out=summed[:], in0=negatives[:], in1=partial, op=ALU.add)
-        negate(3)
-        nc.vector.tensor_tensor(out=product[:], in0=apart, in1=summed[:], op=ALU.mult)
+        nc.vector.tensor_scalar(out=minus_near[:, 3, :], in0=near[:, 3, :], scalar1=-1.0, scalar2=None, op0=ALU.mult)
+        nc.scalar.activation(out=far23[:, 0, :], in_=apart[:, 1, :], func=ACT.Square)
 
         early = [psum.tile([P, H], F32, name=f"early{ft}", tag=f"bank{ft}") for ft in range(2)]
         for ft in range(2):
-            for src in (minus_near, far01):
-                for c in (0, 1):
-                    first = src is minus_near and c == 0
-                    last = src is far01 and c == 1
-                    turn(early[ft][:, P * c : P * (c + 1)], src[:, c, P * ft : P * (ft + 1)], first, last)
-        for src, place in ((minus_near[:, 3, :], 1), (far3[:], 1), (product[:], 0)):
+            terms = ((far0[:], 0), (minus_near[:, 0, :], 0), (minus_near[:, 1, :], 1), (far1[:], 1))
+            for count, (src, c) in enumerate(terms):
+                turn(early[ft][:, P * c : P * (c + 1)], src[:, P * ft : P * (ft + 1)], count == 0, count == len(terms) - 1)
+        terms = ((far23[:, 1, :], 1), (minus_near[:, LONE, :], 0), (minus_near[:, 3, :], 1), (far23[:, 0, :], 0))
+        for count, (src, place) in enumerate(terms):
             for ft in range(2):
-                turn(late[ft][:, P * place : P * (place + 1)], src[:, P * ft : P * (ft + 1)], False, place == 0)
-        for ft in range(2):
-            nc.scalar.activation(out=result_early[ft][:], in_=early[ft][:], func=ACT.Relu, scale=-1.0)
-            nc.sync.dma_start(out=out[P * ft : P * (ft + 1), 0:H], in_=result_early[ft][:])
-        nc.vector.tensor_scalar(out=result_late[0][:], in0=late[0][:], scalar1=-1.0, scalar2=0.0, op0=ALU.mult, op1=ALU.max)
-        nc.sync.dma_start(out=out[0:P, H:V], in_=result_late[0][:])
-        nc.scalar.activation(out=result_late[1][:], in_=late[1][:], func=ACT.Relu, scale=-1.0)
-        nc.scalar.dma_start(out=out[P : 2 * P, H:V], in_=result_late[1][:])
+                turn(late[ft][:, P * place : P * (place + 1)], src[:, P * ft : P * (ft + 1)], False, count == len(terms) - 1)
+        for acc, res, cols in ((early, result_early, slice(0, H)), (late, result_late, slice(H, V))):
+            nc.vector.tensor_scalar(out=res[0][:], in0=acc[0][:], scalar1=-1.0, scalar2=0.0, op0=ALU.mult, op1=ALU.max)
+            nc.sync.dma_start(out=out[0:P, cols], in_=res[0][:])
+            nc.scalar.activation(out=res[1][:], in_=acc[1][:], func=ACT.Relu, scale=-1.0)
+            (nc.sync if acc is early else nc.scalar).dma_start(out=out[P : 2 * P, cols], in_=res[1][:])

@@ -10,7 +10,6 @@ LIST_ROWS = 16
 ANCHOR, POSITIVE, NEGATIVE = 0, 1, 2
 H = V // 2
 LONE = 2
-SPLIT = 448
 FLOPS = 2 * K * N * S
 
 F32 = mybir.dt.float32
@@ -36,9 +35,9 @@ def tile_picked_triplet_none_e_kernel(tc, xT, w1_words, w1_scales, margin, offs,
         identity = keep.tile([P, P], F32, name="identity")
         make_identity(nc, identity[:])
         planes = [keep.tile([P, T], F32, name=f"plane{j}") for j in range(PACK)]
-        dense = [keep.tile([P, S], BF16, name=f"dense{j}", tag=f"dense{j}") for j in range(PACK)]
+        dense = [keep.tile([P, S], BF16, name=f"dense{j}") for j in range(PACK)]
         picked = [keep.tile([P, V, PACK], BF16, name=f"picked{i}", tag=f"picked{i}", align_bytes=64) for i in range(3)]
-        words = {(i, h): keep.tile([P, H], U32, name=f"words{i}{h}", tag=f"words{i}{h}", align_bytes=64) for i in range(3) for h in range(2) if (i, h) != (NEGATIVE, 1)}
+        words = [keep.tile([P, V], U32, name=f"words{i}", align_bytes=64) for i in range(3)]
         scales = [keep.tile([P, V], U8, name=f"scales{i}", align_bytes=64) for i in range(3)]
 
         nc.vector.memset(w_scales[:].bitcast(I32), 0)
@@ -73,28 +72,35 @@ def tile_picked_triplet_none_e_kernel(tc, xT, w1_words, w1_scales, margin, offs,
             copy(out=picked[i][:, v0:v1, j], in_=dense[j][:, i * V + v0 : i * V + v1])
 
         LAST = PACK - 1
+        END = V - P
         for j in range(LAST):
             nc.vector.tensor_copy(out=picked[ANCHOR][:, :, j], in_=planes[j][:].indirect(entries(0, V)))
             gather(POSITIVE, j, 0, 2 * V)
-            weave(nc.vector.tensor_copy, POSITIVE, j, 0, V)
-            if j < 2:
-                weave(nc.vector.tensor_copy, NEGATIVE, j, 0, V)
-            else:
-                weave(nc.vector.tensor_copy, NEGATIVE, j, 0, H)
-                weave(nc.vector.tensor_copy, NEGATIVE, j, SPLIT, V)
-                weave(nc.scalar.copy, NEGATIVE, j, H, SPLIT)
+            for i in (POSITIVE, NEGATIVE):
+                weave(nc.vector.tensor_copy, i, j, 0, V if j < 2 else END)
+        for i in (POSITIVE, NEGATIVE):
+            weave(nc.scalar.copy, i, 2, END, V)
         for v0 in (0, P):
             nc.vector.tensor_copy(out=dense[LAST][:, v0 : v0 + P], in_=planes[LAST][:].indirect(entries(v0, v0 + P)))
-        for i, v0 in ((POSITIVE, 0), (NEGATIVE, 0), (ANCHOR, H), (POSITIVE, H)):
-            gather(i, LAST, v0, v0 + H)
-        for v0 in (H, H + P):
-            gather(NEGATIVE, LAST, v0, v0 + P)
-        for v0, v1 in ((H, H + P), (H + P, SPLIT)):
-            weave(nc.scalar.copy, NEGATIVE, LAST, v0, v1)
+        for i, v0, v1 in (
+            (POSITIVE, 0, H),
+            (ANCHOR, H, V),
+            (NEGATIVE, 0, H),
+            (POSITIVE, H, END),
+            (NEGATIVE, H, END),
+            (POSITIVE, END, V),
+            (NEGATIVE, END, V),
+        ):
+            gather(i, LAST, v0, v1)
+        for i in (POSITIVE, NEGATIVE):
+            weave(nc.scalar.copy, i, LAST, END, V)
+
+        def lay(i, v0, v1):
+            weave(nc.vector.tensor_copy, i, LAST, v0, v1)
 
         def quantise(i, v0, v1):
             nc.vector.quantize_mx(
-                out=words[i, v0 // H][:, v0 % H : v0 % H + v1 - v0].bitcast(FP8X4),
+                out=words[i][:, v0:v1].bitcast(FP8X4),
                 scales=scales[i][:, v0:v1],
                 in_=picked[i][:, v0:v1, :].rearrange("p v j -> p (v j)"),
             )
@@ -102,7 +108,7 @@ def tile_picked_triplet_none_e_kernel(tc, xT, w1_words, w1_scales, margin, offs,
         def project(acc, i, c, start, stop):
             nc.tensor.matmul_mx(
                 out=acc,
-                lhsT=words[i, c // 2][:, P * (c % 2) : P * (c % 2 + 1)].bitcast(FP8X4),
+                lhsT=words[i][:, P * c : P * (c + 1)].bitcast(FP8X4),
                 lhsT_scale=scales[i][:, P * c : P * (c + 1)],
                 rhs=w_words[:].bitcast(FP8X4),
                 rhs_scale=w_scales[:],
@@ -114,68 +120,62 @@ def tile_picked_triplet_none_e_kernel(tc, xT, w1_words, w1_scales, margin, offs,
             nc.tensor.matmul(out=acc, lhsT=src, rhs=identity[:], start=start, stop=stop, is_transpose=True)
 
         minus_margin = keep.tile([P, 4], F32, name="minus_margin")
-        turned_row = psum.tile([P, 4, P], F32, name="turned_row", tag="bank4")
+        turned_row = psum.tile([P, 4, P], F32, name="turned_row", tag="bank2")
         for c in range(4):
             nc.tensor.transpose(turned_row[:, c, :], margin_row[:, P * c : P * (c + 1)], identity[:])
         nc.scalar.activation(out=minus_margin[:], in_=turned_row[:, :, 0], func=ACT.Copy, scale=-1.0)
-        def add_margin(acc, c, start):
-            turn(acc[:, P * (c % 2) : P * (c % 2 + 1)], minus_margin[:, c : c + 1].to_broadcast([P, P]), start, False)
 
         late = [psum.tile([P, H], F32, name=f"late{ft}") for ft in range(2)]
         for ft in range(2):
-            add_margin(late[ft], 2, True)
-            add_margin(late[ft], 3, False)
+            for c in (2, 3):
+                turn(late[ft][:, P * (c - 2) : P * (c - 1)], minus_margin[:, c : c + 1].to_broadcast([P, P]), c == 2, False)
 
         pos01 = psum.tile([P, 2, N], F32, name="pos01", tag="bank0")
         neg01 = psum.tile([P, 2, N], F32, name="neg01", tag="bank1")
-        lone = {i: psum.tile([P, N], F32, name=f"lone{i}", tag=tag) for i, tag in enumerate(("bank2", "bank3", "bank5"))}
-        last = psum.tile([P, 2, N], F32, name="last", tag="bank4")
-        pos3, neg3 = last[:, 0, :], last[:, 1, :]
+        lone_anchor = psum.tile([P, N], F32, name="lone_anchor", tag="bank2")
+        lone_pair = psum.tile([P, 2, N], F32, name="lone_pair", tag="bank3")
+        pos3 = psum.tile([P, N], F32, name="pos3", tag="bank4")
+        neg3 = psum.tile([P, N], F32, name="neg3", tag="bank5")
         anchors = keep.tile([P, N], F32, name="anchors")
         near = keep.tile([P, 4, N], F32, name="near")
-        far23 = keep.tile([P, 2, N], F32, name="far23")
+        far = keep.tile([P, 4, N], F32, name="far")
         result_early = [keep.tile([P, H], F32, name=f"result_early{ft}") for ft in range(2)]
         result_late = [keep.tile([P, H], F32, name=f"result_late{ft}") for ft in range(2)]
 
-        for v0 in (0, P):
-            weave(nc.vector.tensor_copy, ANCHOR, LAST, v0, v0 + P)
+        lay(ANCHOR, 0, P)
+        lay(ANCHOR, P, H)
         quantise(ANCHOR, 0, P)
         quantise(ANCHOR, P, H)
-        project(pos01[:, 0, :], ANCHOR, 0, True, False)
-        project(neg01[:, 0, :], ANCHOR, 0, True, False)
-        project(pos01[:, 1, :], ANCHOR, 1, False, False)
-        weave(nc.vector.tensor_copy, POSITIVE, LAST, 0, H)
-        weave(nc.vector.tensor_copy, NEGATIVE, LAST, 0, H)
+        for acc in (pos01, neg01):
+            for c in (0, 1):
+                project(acc[:, c, :], ANCHOR, c, c == 0, False)
+        lay(POSITIVE, 0, H)
+        lay(ANCHOR, H, V)
         quantise(POSITIVE, 0, H)
-        project(pos01[:, 0, :], POSITIVE, 0, False, False)
-        project(pos01[:, 1, :], POSITIVE, 1, False, True)
-        quantise(NEGATIVE, 0, H)
-        project(neg01[:, 0, :], NEGATIVE, 0, False, False)
-        project(neg01[:, 1, :], NEGATIVE, 1, False, False)
-        project(neg01[:, 1, :], ANCHOR, 1, False, True)
-        weave(nc.vector.tensor_copy, ANCHOR, LAST, H, V)
-        weave(nc.vector.tensor_copy, POSITIVE, LAST, H, V)
+        for c in (0, 1):
+            project(pos01[:, c, :], POSITIVE, c, False, c == 1)
+        lay(NEGATIVE, 0, H)
         quantise(ANCHOR, H, V)
-        project(lone[ANCHOR][:], ANCHOR, LONE, True, True)
-        project(pos3, ANCHOR, 3, True, False)
-        project(neg3, ANCHOR, 3, False, False)
-        weave(nc.vector.tensor_copy, NEGATIVE, LAST, SPLIT, V)
-        quantise(POSITIVE, H, V)
-        project(lone[POSITIVE][:], POSITIVE, LONE, True, True)
-        project(pos3, POSITIVE, 3, False, False)
-        words[NEGATIVE, 1] = keep.tile([P, H], U32, name="words_last", tag=f"picked{ANCHOR}", align_bytes=64)
-        quantise(NEGATIVE, H, V)
-        project(lone[NEGATIVE][:], NEGATIVE, LONE, True, True)
-        project(neg3, NEGATIVE, 3, False, True)
+        project(lone_anchor[:], ANCHOR, LONE, True, True)
+        project(pos3[:], ANCHOR, 3, True, False)
+        project(neg3[:], ANCHOR, 3, True, False)
+        lay(POSITIVE, H, END)
+        quantise(NEGATIVE, 0, H)
+        for c in (0, 1):
+            project(neg01[:, c, :], NEGATIVE, c, False, c == 1)
+        lay(NEGATIVE, H, END)
+        for place, i in enumerate((POSITIVE, NEGATIVE)):
+            quantise(i, H, END)
+            project(lone_pair[:, place, :], i, LONE, True, True)
+        for acc, i in ((pos3, POSITIVE), (neg3, NEGATIVE)):
+            quantise(i, END, V)
+            project(acc[:], i, 3, False, True)
 
         nc.scalar.activation(out=near[:, 0:2, :], in_=pos01[:], func=ACT.Square)
-        far0 = keep.tile([P, N], F32, name="far0")
-        nc.scalar.activation(out=far0[:], in_=neg01[:, 0, :], func=ACT.Square)
-        nc.scalar.copy(out=anchors[:], in_=lone[ANCHOR][:])
-        far1 = keep.tile([P, N], F32, name="far1", tag=f"words{ANCHOR}1", align_bytes=64)
-        nc.scalar.activation(out=far1[:], in_=neg01[:, 1, :], func=ACT.Square)
-        nc.scalar.activation(out=near[:, 3, :], in_=pos3, func=ACT.Square)
-        nc.scalar.activation(out=far23[:, 1, :], in_=neg3, func=ACT.Square)
+        nc.scalar.copy(out=anchors[:], in_=lone_anchor[:])
+        nc.scalar.activation(out=far[:, 0:2, :], in_=neg01[:], func=ACT.Square)
+        nc.scalar.activation(out=near[:, 3, :], in_=pos3[:], func=ACT.Square)
+        nc.scalar.activation(out=far[:, 3, :], in_=neg3[:], func=ACT.Square)
 
         minus_near = keep.tile([P, 4, N], F32, name="minus_near", tag=f"picked{POSITIVE}", align_bytes=64)
         apart = keep.tile([P, 2, N], F32, name="apart", tag=f"picked{NEGATIVE}", align_bytes=64)
@@ -183,23 +183,23 @@ def tile_picked_triplet_none_e_kernel(tc, xT, w1_words, w1_scales, margin, offs,
             nc.vector.tensor_scalar(
                 out=minus_near[:, c, :], in0=near[:, c, :], scalar1=-1.0, scalar2=minus_margin[:, c : c + 1], op0=ALU.mult, op1=ALU.add
             )
-        for place, i in enumerate((POSITIVE, NEGATIVE)):
-            nc.vector.tensor_tensor(out=apart[:, place, :], in0=lone[i][:], in1=anchors[:], op=ALU.add)
+        for place in range(2):
+            nc.vector.tensor_tensor(out=apart[:, place, :], in0=lone_pair[:, place, :], in1=anchors[:], op=ALU.add)
         nc.vector.scalar_tensor_tensor(
             out=minus_near[:, LONE, :], in0=apart[:, 0, :], scalar=-1.0, in1=apart[:, 0, :], op0=ALU.mult, op1=ALU.mult
         )
         nc.vector.tensor_scalar(out=minus_near[:, 3, :], in0=near[:, 3, :], scalar1=-1.0, scalar2=None, op0=ALU.mult)
-        nc.scalar.activation(out=far23[:, 0, :], in_=apart[:, 1, :], func=ACT.Square)
+        nc.scalar.activation(out=far[:, LONE, :], in_=apart[:, 1, :], func=ACT.Square)
 
-        early = [psum.tile([P, H], F32, name=f"early{ft}", tag=f"bank{ft}") for ft in range(2)]
-        for ft in range(2):
-            terms = ((far0[:], 0), (minus_near[:, 0, :], 0), (minus_near[:, 1, :], 1), (far1[:], 1))
-            for count, (src, c) in enumerate(terms):
-                turn(early[ft][:, P * c : P * (c + 1)], src[:, P * ft : P * (ft + 1)], count == 0, count == len(terms) - 1)
-        terms = ((far23[:, 1, :], 1), (minus_near[:, LONE, :], 0), (minus_near[:, 3, :], 1), (far23[:, 0, :], 0))
-        for count, (src, place) in enumerate(terms):
+        early = [psum.tile([P, H], F32, name=f"early{ft}", tag=tag) for ft, tag in enumerate(("bank0", "bank2"))]
+        for term in (minus_near, far):
             for ft in range(2):
-                turn(late[ft][:, P * place : P * (place + 1)], src[:, P * ft : P * (ft + 1)], False, count == len(terms) - 1)
+                for c in (0, 1):
+                    turn(early[ft][:, P * c : P * (c + 1)], term[:, c, P * ft : P * (ft + 1)], term is minus_near and c == 0, term is far and c == 1)
+        terms = ((far, 3), (minus_near, LONE), (minus_near, 3), (far, LONE))
+        for count, (term, c) in enumerate(terms):
+            for ft in range(2):
+                turn(late[ft][:, P * (c - 2) : P * (c - 1)], term[:, c, P * ft : P * (ft + 1)], False, count == len(terms) - 1)
         for acc, res, cols in ((early, result_early, slice(0, H)), (late, result_late, slice(H, V))):
             nc.vector.tensor_scalar(out=res[0][:], in0=acc[0][:], scalar1=-1.0, scalar2=0.0, op0=ALU.mult, op1=ALU.max)
             nc.sync.dma_start(out=out[0:P, cols], in_=res[0][:])

@@ -116,39 +116,55 @@ def tile_picked_triplet_none_e_kernel(tc, xT, w1_words, w1_scales, margin, offs,
                 stop=stop,
             )
 
+        def project_turned(acc, i, c, start, stop):
+            for ft in range(2):
+                nc.tensor.matmul_mx(
+                    out=acc[:, ft, :],
+                    lhsT=w_words[:, P * ft : P * (ft + 1)].bitcast(FP8X4),
+                    lhsT_scale=w_scales[:, P * ft : P * (ft + 1)],
+                    rhs=words[i][:, P * c : P * (c + 1)].bitcast(FP8X4),
+                    rhs_scale=scales[i][:, P * c : P * (c + 1)],
+                    start=start and ft == 0,
+                    stop=stop and ft == 1,
+                )
+
         def turn(acc, src, start, stop):
             nc.tensor.matmul(out=acc, lhsT=src, rhs=identity[:], start=start, stop=stop, is_transpose=True)
 
-        minus_margin = keep.tile([P, 4], F32, name="minus_margin")
+        minus_margin = keep.tile([P, 3], F32, name="minus_margin")
         turned_row = psum.tile([P, 4, P], F32, name="turned_row", tag="bank2")
         for c in range(4):
             nc.tensor.transpose(turned_row[:, c, :], margin_row[:, P * c : P * (c + 1)], identity[:])
-        nc.scalar.activation(out=minus_margin[:], in_=turned_row[:, :, 0], func=ACT.Copy, scale=-1.0)
+        nc.scalar.activation(out=minus_margin[:], in_=turned_row[:, 0:3, 0], func=ACT.Copy, scale=-1.0)
 
-        late = [psum.tile([P, H], F32, name=f"late{ft}") for ft in range(2)]
+        margin3 = keep.tile([P, 1], F32, name="margin3")
+        nc.scalar.copy(out=margin3[:], in_=turned_row[:, 3, 0:1])
+
+        minus_loss2 = psum.tile([P, 2, P], F32, name="minus_loss2")
+        near_sum3 = psum.tile([P, 2, P], F32, name="near_sum3")
         for ft in range(2):
-            for c in (2, 3):
-                turn(late[ft][:, P * (c - 2) : P * (c - 1)], minus_margin[:, c : c + 1].to_broadcast([P, P]), c == 2, False)
+            turn(minus_loss2[:, ft, :], minus_margin[:, LONE : LONE + 1].to_broadcast([P, P]), ft == 0, False)
+            turn(near_sum3[:, ft, :], margin3[:].to_broadcast([P, P]), ft == 0, False)
 
         pos01 = psum.tile([P, 2, N], F32, name="pos01", tag="bank0")
         neg01 = psum.tile([P, 2, N], F32, name="neg01", tag="bank1")
         lone_anchor = psum.tile([P, N], F32, name="lone_anchor", tag="bank2")
         lone_pair = psum.tile([P, 2, N], F32, name="lone_pair", tag="bank3")
         pos3 = psum.tile([P, N], F32, name="pos3", tag="bank4")
-        neg3 = psum.tile([P, N], F32, name="neg3", tag="bank5")
+        neg3 = psum.tile([P, 2, P], F32, name="neg3", tag="bank5")
         anchors = keep.tile([P, N], F32, name="anchors")
         near = keep.tile([P, 4, N], F32, name="near")
         far = keep.tile([P, 4, N], F32, name="far")
         result_early = [keep.tile([P, H], F32, name=f"result_early{ft}") for ft in range(2)]
-        result_late = [keep.tile([P, H], F32, name=f"result_late{ft}") for ft in range(2)]
+        result_late = keep.tile([P, 2, H], F32, name="result_late")
 
         lay(ANCHOR, 0, P)
         lay(ANCHOR, P, H)
         quantise(ANCHOR, 0, P)
         quantise(ANCHOR, P, H)
-        for acc in (pos01, neg01):
-            for c in (0, 1):
-                project(acc[:, c, :], ANCHOR, c, c == 0, False)
+        project(pos01[:, 0, :], ANCHOR, 0, True, False)
+        project(neg01[:, 0, :], ANCHOR, 0, True, False)
+        project(pos01[:, 1, :], ANCHOR, 1, False, False)
         lay(POSITIVE, 0, H)
         lay(ANCHOR, H, V)
         quantise(POSITIVE, 0, H)
@@ -158,26 +174,28 @@ def tile_picked_triplet_none_e_kernel(tc, xT, w1_words, w1_scales, margin, offs,
         quantise(ANCHOR, H, V)
         project(lone_anchor[:], ANCHOR, LONE, True, True)
         project(pos3[:], ANCHOR, 3, True, False)
-        project(neg3[:], ANCHOR, 3, True, False)
+        project_turned(neg3, ANCHOR, 3, True, False)
         lay(POSITIVE, H, END)
         quantise(NEGATIVE, 0, H)
         for c in (0, 1):
-            project(neg01[:, c, :], NEGATIVE, c, False, c == 1)
+            project(neg01[:, c, :], NEGATIVE, c, False, False)
+        project(neg01[:, 1, :], ANCHOR, 1, False, True)
         lay(NEGATIVE, H, END)
         for place, i in enumerate((POSITIVE, NEGATIVE)):
             quantise(i, H, END)
             project(lone_pair[:, place, :], i, LONE, True, True)
-        for acc, i in ((pos3, POSITIVE), (neg3, NEGATIVE)):
-            quantise(i, END, V)
-            project(acc[:], i, 3, False, True)
+        quantise(POSITIVE, END, V)
+        project(pos3[:], POSITIVE, 3, False, True)
+        quantise(NEGATIVE, END, V)
+        project_turned(neg3, NEGATIVE, 3, False, True)
 
         nc.scalar.activation(out=near[:, 0:2, :], in_=pos01[:], func=ACT.Square)
         nc.scalar.copy(out=anchors[:], in_=lone_anchor[:])
         nc.scalar.activation(out=far[:, 0:2, :], in_=neg01[:], func=ACT.Square)
         nc.scalar.activation(out=near[:, 3, :], in_=pos3[:], func=ACT.Square)
-        nc.scalar.activation(out=far[:, 3, :], in_=neg3[:], func=ACT.Square)
+        nc.scalar.activation(out=far[:, 3, :], in_=neg3[:].rearrange("p f v -> p (f v)"), func=ACT.Square)
 
-        minus_near = keep.tile([P, 4, N], F32, name="minus_near", tag=f"picked{POSITIVE}", align_bytes=64)
+        minus_near = keep.tile([P, 3, N], F32, name="minus_near", tag=f"picked{POSITIVE}", align_bytes=64)
         apart = keep.tile([P, 2, N], F32, name="apart", tag=f"picked{NEGATIVE}", align_bytes=64)
         for c in (0, 1):
             nc.vector.tensor_scalar(
@@ -188,20 +206,33 @@ def tile_picked_triplet_none_e_kernel(tc, xT, w1_words, w1_scales, margin, offs,
         nc.vector.scalar_tensor_tensor(
             out=minus_near[:, LONE, :], in0=apart[:, 0, :], scalar=-1.0, in1=apart[:, 0, :], op0=ALU.mult, op1=ALU.mult
         )
-        nc.vector.tensor_scalar(out=minus_near[:, 3, :], in0=near[:, 3, :], scalar1=-1.0, scalar2=None, op0=ALU.mult)
         nc.scalar.activation(out=far[:, LONE, :], in_=apart[:, 1, :], func=ACT.Square)
 
         early = [psum.tile([P, H], F32, name=f"early{ft}", tag=tag) for ft, tag in enumerate(("bank0", "bank2"))]
-        for term in (minus_near, far):
+
+        def add_early(term, ft):
+            for c in (0, 1):
+                turn(early[ft][:, P * c : P * (c + 1)], term[:, c, P * ft : P * (ft + 1)], term is minus_near and c == 0, term is far and c == 1)
+
+        def add_late(acc, term, c, stop):
             for ft in range(2):
-                for c in (0, 1):
-                    turn(early[ft][:, P * c : P * (c + 1)], term[:, c, P * ft : P * (ft + 1)], term is minus_near and c == 0, term is far and c == 1)
-        terms = ((far, 3), (minus_near, LONE), (minus_near, 3), (far, LONE))
-        for count, (term, c) in enumerate(terms):
-            for ft in range(2):
-                turn(late[ft][:, P * (c - 2) : P * (c - 1)], term[:, c, P * ft : P * (ft + 1)], False, count == len(terms) - 1)
-        for acc, res, cols in ((early, result_early, slice(0, H)), (late, result_late, slice(H, V))):
-            nc.vector.tensor_scalar(out=res[0][:], in0=acc[0][:], scalar1=-1.0, scalar2=0.0, op0=ALU.mult, op1=ALU.max)
-            nc.sync.dma_start(out=out[0:P, cols], in_=res[0][:])
-            nc.scalar.activation(out=res[1][:], in_=acc[1][:], func=ACT.Relu, scale=-1.0)
-            (nc.sync if acc is early else nc.scalar).dma_start(out=out[P : 2 * P, cols], in_=res[1][:])
+                turn(acc[:, ft, :], term[:, c, P * ft : P * (ft + 1)], False, stop and ft == 1)
+
+        add_early(minus_near, 0)
+        add_early(minus_near, 1)
+        add_early(far, 0)
+        add_late(near_sum3, near, 3, True)
+        add_early(far, 1)
+        add_late(minus_loss2, minus_near, LONE, False)
+        add_late(minus_loss2, far, LONE, True)
+
+        nc.vector.tensor_scalar(out=result_early[0][:], in0=early[0][:], scalar1=-1.0, scalar2=0.0, op0=ALU.mult, op1=ALU.max)
+        nc.sync.dma_start(out=out[0:P, 0:H], in_=result_early[0][:])
+        nc.scalar.activation(out=result_early[1][:], in_=early[1][:], func=ACT.Relu, scale=-1.0)
+        nc.sync.dma_start(out=out[P : 2 * P, 0:H], in_=result_early[1][:])
+        loss3 = keep.tile([P, 2, P], F32, name="loss3")
+        nc.vector.tensor_tensor(out=loss3[:], in0=near_sum3[:], in1=far[:, 3, :].rearrange("p (f v) -> p f v", f=2), op=ALU.subtract)
+        nc.vector.tensor_scalar(out=result_late[:, :, P:H], in0=loss3[:], scalar1=0.0, scalar2=None, op0=ALU.max)
+        nc.scalar.activation(out=result_late[:, :, 0:P], in_=minus_loss2[:], func=ACT.Relu, scale=-1.0)
+        nc.sync.dma_start(out=out[0:P, H:V], in_=result_late[:, 0, :])
+        nc.scalar.dma_start(out=out[P : 2 * P, H:V], in_=result_late[:, 1, :])

@@ -48,9 +48,9 @@ def tile_picked_triplet_none_e_kernel(tc, xT, w1_words, w1_scales, margin, offs,
             nc.sync.dma_start(out=planes[j][:], in_=rows[j])
             if j == 0:
                 nc.sync.dma_start(offsets[:], offs)
-                nc.sync.dma_start(out=margin_row[0:1, :], in_=margin[0:1, :])
+                nc.scalar.dma_start(out=margin_row[0:1, :], in_=margin[0:1, :])
                 for q in range(P // 32):
-                    nc.sync.dma_start(
+                    nc.scalar.dma_start(
                         out=w_scales[32 * q : 32 * q + 4, :].bitcast(I32),
                         in_=w1_scales[0, 4 * q : 4 * q + 4, :].bitcast(I32),
                     )

@@ -234,5 +234,4 @@ def tile_picked_triplet_none_e_kernel(tc, xT, w1_words, w1_scales, margin, offs,
         nc.vector.tensor_tensor(out=loss3[:], in0=near_sum3[:], in1=far[:, 3, :].rearrange("p (f v) -> p f v", f=2), op=ALU.subtract)
         nc.vector.tensor_scalar(out=result_late[:, :, P:H], in0=loss3[:], scalar1=0.0, scalar2=None, op0=ALU.max)
         nc.scalar.activation(out=result_late[:, :, 0:P], in_=minus_loss2[:], func=ACT.Relu, scale=-1.0)
-        nc.sync.dma_start(out=out[0:P, H:V], in_=result_late[:, 0, :])
-        nc.scalar.dma_start(out=out[P : 2 * P, H:V], in_=result_late[:, 1, :])
+        nc.sync.dma_start(out=out[:, H:V].rearrange("(f p) v -> p f v", f=2), in_=result_late[:])

from contextlib import ExitStack

import concourse.mybir as mybir
from concourse.masks import make_identity

K, T, S, V, N = 512, 4096, 1536, 512, 256
P = 128
PACK = 4
LIST_ROWS = 16
ANCHOR, POSITIVE, NEGATIVE = 0, 1, 2
H = V // 2
LONE = 2
FLOPS = 2 * K * N * S

F32 = mybir.dt.float32
BF16 = mybir.dt.bfloat16
I32 = mybir.dt.int32
U32 = mybir.dt.uint32
U16 = mybir.dt.uint16
U8 = mybir.dt.uint8
FP8X4 = mybir.dt.float8_e4m3fn_x4
ACT = mybir.ActivationFunctionType
ALU = mybir.AluOpType


def tile_picked_triplet_none_e_kernel(tc, xT, w1_words, w1_scales, margin, offs, out):
    nc = tc.nc
    with ExitStack() as ctx:
        keep = ctx.enter_context(tc.tile_pool(name="keep", bufs=1))
        psum = ctx.enter_context(tc.psum_pool(name="psum", bufs=1))

        offsets = keep.tile([P, S // LIST_ROWS], U16, name="offsets")
        w_words = keep.tile([P, N], U32, name="w_words", align_bytes=64)
        w_scales = keep.tile([P, N], U8, name="w_scales", align_bytes=64)
        identity = keep.tile([P, P], F32, name="identity")
        make_identity(nc, identity[:])
        planes = [keep.tile([P, T], F32, name=f"plane{j}") for j in range(PACK)]
        dense = [keep.tile([P, S], BF16, name=f"dense{j}") for j in range(PACK)]
        picked = [keep.tile([P, V, PACK], BF16, name=f"picked{i}", tag=f"picked{i}", align_bytes=64) for i in range(3)]
        words = [keep.tile([P, V], U32, name=f"words{i}", align_bytes=64) for i in range(3)]
        scales = [keep.tile([P, V], U8, name=f"scales{i}", align_bytes=64) for i in range(3)]

        nc.vector.memset(w_scales[:].bitcast(I32), 0)
        margin_row = keep.tile([P, V], F32, name="margin_row")
        nc.vector.memset(margin_row[:], 0.0)
        rows = xT.rearrange("(p j) t -> j p t", j=PACK)
        for j in range(PACK):
            nc.sync.dma_start(out=planes[j][:], in_=rows[j])
            if j == 0:
                nc.sync.dma_start(offsets[:], offs)
                nc.scalar.dma_start(out=margin_row[0:1, :], in_=margin[0:1, :])
                for q in range(P // 32):
                    nc.scalar.dma_start(
                        out=w_scales[32 * q : 32 * q + 4, :].bitcast(I32),
                        in_=w1_scales[0, 4 * q : 4 * q + 4, :].bitcast(I32),
                    )
        nc.sync.dma_start(out=w_words[:].bitcast(I32), in_=w1_words[0].rearrange("p n t -> p (n t)").bitcast(I32))

        def entries(s0, s1):
            return offsets[:, s0 // LIST_ROWS : s1 // LIST_ROWS]

        def gather(i, j, v0, v1):
            s0, s1 = i * V + v0, i * V + v1
            nc.scalar.activation(
                out=dense[j][:, s0:s1],
                in_=planes[j][:].indirect(entries(s0, s1)),
                func=ACT.Copy,
                scale=1.0 if i == ANCHOR else -1.0,
            )

        def weave(copy, i, j, v0, v1):
            copy(out=picked[i][:, v0:v1, j], in_=dense[j][:, i * V + v0 : i * V + v1])

        LAST = PACK - 1
        END = V - P
        for j in range(LAST):
            nc.vector.tensor_copy(out=picked[ANCHOR][:, :, j], in_=planes[j][:].indirect(entries(0, V)))
            gather(POSITIVE, j, 0, 2 * V)
            for i in (POSITIVE, NEGATIVE):
                weave(nc.vector.tensor_copy, i, j, 0, V if j < 2 else END)
        for i in (POSITIVE, NEGATIVE):
            weave(nc.scalar.copy, i, 2, END, V)
        for v0 in (0, P):
            nc.vector.tensor_copy(out=dense[LAST][:, v0 : v0 + P], in_=planes[LAST][:].indirect(entries(v0, v0 + P)))
        for i, v0, v1 in (
            (POSITIVE, 0, H),
            (ANCHOR, H, V),
            (NEGATIVE, 0, H),
            (POSITIVE, H, END),
            (NEGATIVE, H, END),
            (POSITIVE, END, V),
            (NEGATIVE, END, V),
        ):
            gather(i, LAST, v0, v1)
        for i in (POSITIVE, NEGATIVE):
            weave(nc.scalar.copy, i, LAST, END, V)

        def lay(i, v0, v1):
            weave(nc.vector.tensor_copy, i, LAST, v0, v1)

        def quantise(i, v0, v1):
            nc.vector.quantize_mx(
                out=words[i][:, v0:v1].bitcast(FP8X4),
                scales=scales[i][:, v0:v1],
                in_=picked[i][:, v0:v1, :].rearrange("p v j -> p (v j)"),
            )

        def project(acc, i, c, start, stop):
            nc.tensor.matmul_mx(
                out=acc,
                lhsT=words[i][:, P * c : P * (c + 1)].bitcast(FP8X4),
                lhsT_scale=scales[i][:, P * c : P * (c + 1)],
                rhs=w_words[:].bitcast(FP8X4),
                rhs_scale=w_scales[:],
                start=start,
                stop=stop,
            )

        def project_turned(acc, i, c, start, stop):
            for ft in range(2):
                nc.tensor.matmul_mx(
                    out=acc[:, ft, :],
                    lhsT=w_words[:, P * ft : P * (ft + 1)].bitcast(FP8X4),
                    lhsT_scale=w_scales[:, P * ft : P * (ft + 1)],
                    rhs=words[i][:, P * c : P * (c + 1)].bitcast(FP8X4),
                    rhs_scale=scales[i][:, P * c : P * (c + 1)],
                    start=start and ft == 0,
                    stop=stop and ft == 1,
                )

        def turn(acc, src, start, stop):
            nc.tensor.matmul(out=acc, lhsT=src, rhs=identity[:], start=start, stop=stop, is_transpose=True)

        minus_margin = keep.tile([P, 3], F32, name="minus_margin")
        turned_row = psum.tile([P, 4, P], F32, name="turned_row", tag="bank2")
        for c in range(4):
            nc.tensor.transpose(turned_row[:, c, :], margin_row[:, P * c : P * (c + 1)], identity[:])
        nc.scalar.activation(out=minus_margin[:], in_=turned_row[:, 0:3, 0], func=ACT.Copy, scale=-1.0)

        margin3 = keep.tile([P, 1], F32, name="margin3")
        nc.scalar.copy(out=margin3[:], in_=turned_row[:, 3, 0:1])

        minus_loss2 = psum.tile([P, 2, P], F32, name="minus_loss2")
        near_sum3 = psum.tile([P, 2, P], F32, name="near_sum3")
        for ft in range(2):
            turn(minus_loss2[:, ft, :], minus_margin[:, LONE : LONE + 1].to_broadcast([P, P]), ft == 0, False)
            turn(near_sum3[:, ft, :], margin3[:].to_broadcast([P, P]), ft == 0, False)

        pos01 = psum.tile([P, 2, N], F32, name="pos01", tag="bank0")
        neg01 = psum.tile([P, 2, N], F32, name="neg01", tag="bank1")
        lone_anchor = psum.tile([P, N], F32, name="lone_anchor", tag="bank2")
        lone_pair = psum.tile([P, 2, N], F32, name="lone_pair", tag="bank3")
        pos3 = psum.tile([P, N], F32, name="pos3", tag="bank4")
        neg3 = psum.tile([P, 2, P], F32, name="neg3", tag="bank5")
        anchors = keep.tile([P, N], F32, name="anchors")
        near = keep.tile([P, 4, N], F32, name="near")
        far = keep.tile([P, 4, N], F32, name="far")
        result_early = [keep.tile([P, H], F32, name=f"result_early{ft}") for ft in range(2)]
        result_late = keep.tile([P, 2, H], F32, name="result_late")

        lay(ANCHOR, 0, P)
        lay(ANCHOR, P, H)
        quantise(ANCHOR, 0, P)
        quantise(ANCHOR, P, H)
        project(pos01[:, 0, :], ANCHOR, 0, True, False)
        project(neg01[:, 0, :], ANCHOR, 0, True, False)
        project(pos01[:, 1, :], ANCHOR, 1, False, False)
        lay(POSITIVE, 0, H)
        lay(ANCHOR, H, V)
        quantise(POSITIVE, 0, H)
        for c in (0, 1):
            project(pos01[:, c, :], POSITIVE, c, False, c == 1)
        lay(NEGATIVE, 0, H)
        quantise(ANCHOR, H, V)
        project(lone_anchor[:], ANCHOR, LONE, True, True)
        project(pos3[:], ANCHOR, 3, True, False)
        project_turned(neg3, ANCHOR, 3, True, False)
        lay(POSITIVE, H, END)
        quantise(NEGATIVE, 0, H)
        for c in (0, 1):
            project(neg01[:, c, :], NEGATIVE, c, False, False)
        project(neg01[:, 1, :], ANCHOR, 1, False, True)
        lay(NEGATIVE, H, END)
        for place, i in enumerate((POSITIVE, NEGATIVE)):
            quantise(i, H, END)
            project(lone_pair[:, place, :], i, LONE, True, True)
        quantise(POSITIVE, END, V)
        project(pos3[:], POSITIVE, 3, False, True)
        quantise(NEGATIVE, END, V)
        project_turned(neg3, NEGATIVE, 3, False, True)

        nc.scalar.activation(out=near[:, 0:2, :], in_=pos01[:], func=ACT.Square)
        nc.scalar.copy(out=anchors[:], in_=lone_anchor[:])
        nc.scalar.activation(out=far[:, 0:2, :], in_=neg01[:], func=ACT.Square)
        nc.scalar.activation(out=near[:, 3, :], in_=pos3[:], func=ACT.Square)
        nc.scalar.activation(out=far[:, 3, :], in_=neg3[:].rearrange("p f v -> p (f v)"), func=ACT.Square)

        minus_near = keep.tile([P, 3, N], F32, name="minus_near", tag=f"picked{POSITIVE}", align_bytes=64)
        apart = keep.tile([P, 2, N], F32, name="apart", tag=f"picked{NEGATIVE}", align_bytes=64)
        for c in (0, 1):
            nc.vector.tensor_scalar(
                out=minus_near[:, c, :], in0=near[:, c, :], scalar1=-1.0, scalar2=minus_margin[:, c : c + 1], op0=ALU.mult, op1=ALU.add
            )
        for place in range(2):
            nc.vector.tensor_tensor(out=apart[:, place, :], in0=lone_pair[:, place, :], in1=anchors[:], op=ALU.add)
        nc.vector.scalar_tensor_tensor(
            out=minus_near[:, LONE, :], in0=apart[:, 0, :], scalar=-1.0, in1=apart[:, 0, :], op0=ALU.mult, op1=ALU.mult
        )
        nc.scalar.activation(out=far[:, LONE, :], in_=apart[:, 1, :], func=ACT.Square)

        early = [psum.tile([P, H], F32, name=f"early{ft}", tag=tag) for ft, tag in enumerate(("bank0", "bank2"))]

        def add_early(term, ft):
            for c in (0, 1):
                turn(early[ft][:, P * c : P * (c + 1)], term[:, c, P * ft : P * (ft + 1)], term is minus_near and c == 0, term is far and c == 1)

        def add_late(acc, term, c, stop):
            for ft in range(2):
                turn(acc[:, ft, :], term[:, c, P * ft : P * (ft + 1)], False, stop and ft == 1)

        add_early(minus_near, 0)
        add_early(minus_near, 1)
        add_early(far, 0)
        add_late(near_sum3, near, 3, True)
        add_early(far, 1)
        add_late(minus_loss2, minus_near, LONE, False)
        add_late(minus_loss2, far, LONE, True)

        nc.vector.tensor_scalar(out=result_early[0][:], in0=early[0][:], scalar1=-1.0, scalar2=0.0, op0=ALU.mult, op1=ALU.max)
        nc.sync.dma_start(out=out[0:P, 0:H], in_=result_early[0][:])
        nc.scalar.activation(out=result_early[1][:], in_=early[1][:], func=ACT.Relu, scale=-1.0)
        nc.sync.dma_start(out=out[P : 2 * P, 0:H], in_=result_early[1][:])
        loss3 = keep.tile([P, 2, P], F32, name="loss3")
        nc.vector.tensor_tensor(out=loss3[:], in0=near_sum3[:], in1=far[:, 3, :].rearrange("p (f v) -> p f v", f=2), op=ALU.subtract)
        nc.vector.tensor_scalar(out=result_late[:, :, P:H], in0=loss3[:], scalar1=0.0, scalar2=None, op0=ALU.max)
        nc.scalar.activation(out=result_late[:, :, 0:P], in_=minus_loss2[:], func=ACT.Relu, scale=-1.0)
        nc.sync.dma_start(out=out[:, H:V].rearrange("(f p) v -> p f v", f=2), in_=result_late[:])
